import numpy as np
import ml_dtypes


def mxq(x, axis, fmt="e4m3"):
    dtype, down = {"e4m3": (ml_dtypes.float8_e4m3fn, 7), "e5m2": (ml_dtypes.float8_e5m2, 14)}[fmt]
    v = np.moveaxis(np.asarray(x, np.float32).astype(ml_dtypes.bfloat16).astype(np.float64), axis, -1)
    blocks = v.reshape(v.shape[:-1] + (-1, 32))
    amax = np.abs(blocks).max(-1, keepdims=True)
    byte = np.maximum(np.where(amax > 0, np.frexp(amax)[1] - 1 + 127, 0) - down, 1)
    scale = np.exp2(byte - 127.0)
    codes = (blocks / scale).astype(np.float32).astype(dtype).astype(np.float64)
    return np.moveaxis((codes * scale).reshape(v.shape), -1, axis)


WIDE = False


def mx_kscale(k):
    if not WIDE:
        return np.ones(k)
    levels = np.array([30, -30])
    if k % 512:
        return np.exp2(np.random.permutation(np.resize(levels, k // 32))).repeat(32)
    a = np.empty((k // 512, 16))
    for p in range(k // 512):
        a[p, :8] = np.random.permutation(np.resize(levels, 8))
        for g in range(8):
            far = levels[np.abs(levels - a[p, g]) >= 10]
            a[p, g + 8] = far[np.random.randint(len(far))]
    return np.exp2(a.ravel()).repeat(32)


BF16 = ml_dtypes.bfloat16


def bf(x):
    return np.asarray(x, np.float32).astype(BF16)


def f64(x):
    return np.asarray(x).astype(np.float64)


E2M1 = np.array([0.0, 0.5, 1.0, 1.5, 2.0, 3.0, 4.0, 6.0, -0.0, -0.5, -1.0, -1.5, -2.0, -3.0, -4.0, -6.0])


def pack_weight(w, fmt):
    k, n = w.shape
    w = f64(bf(w)).reshape(k // 32, 32, n)
    amax = np.abs(w).max(1)
    if fmt == "e4m3":
        byte = np.frexp(amax)[1] - 1 + 127 - 7
    else:
        mant, ex = np.frexp(amax / 6.0)
        byte = np.where(mant > 0.5, ex, ex - 1) + 127
    byte = np.clip(np.where(amax > 0, byte, 1), 1, 254)
    scaled = (w * np.exp2(127.0 - byte)[:, None, :]).reshape(k, n).astype(np.float32)
    by_word = np.ascontiguousarray(scaled.reshape(k // 512, 128, 4, n).transpose(0, 1, 3, 2))
    if fmt == "e4m3":
        words = by_word.astype(ml_dtypes.float8_e4m3fn).view(np.uint8)
    else:
        c = by_word.astype(ml_dtypes.float4_e2m1fn).view(np.uint8) & 0xF
        words = c[..., 0::2] | (c[..., 1::2] << 4)
    return np.ascontiguousarray(words), np.ascontiguousarray(byte.astype(np.uint8).reshape(k // 512, 16, n))


def unpack_weight(words, scales, fmt):
    g, p, n, _ = words.shape
    if fmt == "e4m3":
        vals = np.ascontiguousarray(words).view(ml_dtypes.float8_e4m3fn).astype(np.float64)
    else:
        nib = np.empty((g, p, n, 4), np.uint8)
        nib[..., 0::2] = words & 0xF
        nib[..., 1::2] = words >> 4
        vals = E2M1[nib]
    vals = vals * np.repeat(np.exp2(scales.astype(np.float64) - 127.0), 8, axis=1)[..., None]
    return vals.transpose(0, 1, 3, 2).reshape(g * 512, n)
def pack4(w):
    words, scales = pack_weight(w, "e2m1")
    return words.reshape(words.shape[0], 128, -1), scales


def unpack4(words, scales):
    return unpack_weight(words.reshape(words.shape[0], 128, -1, 2), scales, "e2m1")


D, K, T, NQ = 1024, 1024, 2048, 512
K1, B = 1.2, 0.75


def setup_inputs():
    s = mx_kscale(K)
    t = mx_kscale(T)
    e_words, e_scales = pack4(np.random.standard_normal((K, T)) / np.sqrt(K) / s[:, None])
    length = np.exp(0.5 * np.random.standard_normal(D))
    rarity = np.exp(0.5 * np.random.standard_normal(T))
    return {"docs": bf(np.random.standard_normal((D, K)) * s),
            "e_words": e_words,
            "e_scales": e_scales,
            "norm": bf(K1 * (1 - B + B * length)),
            "idf": bf((K1 + 1) * rarity * t),
            "queries": bf(np.random.standard_normal((T, NQ)) / np.sqrt(T) / t[:, None])}


def reference(docs, e_words, e_scales, norm, idf, queries):
    e = unpack4(e_words, e_scales)
    tf = np.maximum(mxq(f64(docs), 1, "e4m3") @ e, 0.0)
    impact = f64(idf) * (tf / (tf + f64(norm)[:, None]))
    return mxq(impact, 1, "e5m2") @ mxq(f64(queries), 0, "e4m3")

@@ -1,0 +1,317 @@
+from contextlib import ExitStack
+
+import concourse.mybir as mybir
+from concourse.masks import make_identity
+
+D, K, T, NQ = 1024, 1024, 2048, 512
+FLOPS = 2 * D * K * T + 2 * D * T * NQ
+
+F32 = mybir.dt.float32
+BF16 = mybir.dt.bfloat16
+I32 = mybir.dt.int32
+U32 = mybir.dt.uint32
+U8 = mybir.dt.uint8
+E4M3 = mybir.dt.float8_e4m3fn_x4
+E5M2 = mybir.dt.float8_e5m2_x4
+E2M1 = mybir.dt.float4_e2m1fn_x4
+ALU = mybir.AluOpType
+ACT = mybir.ActivationFunctionType
+
+P = 128
+KP = K // 512
+TP = T // 512
+DT = D // P
+PAIR = 2
+UNITS = (DT // PAIR) * TP
+
+
+def tile_learned_bm25_scores_s9_kernel(tc, docs, e_words, e_scales, norm, idf, queries, out):
+    nc = tc.nc
+    with ExitStack() as ctx:
+        keep = ctx.enter_context(tc.tile_pool(name="keep", bufs=1))
+        work = ctx.enter_context(tc.tile_pool(name="work", bufs=3))
+        psum = ctx.enter_context(tc.psum_pool(name="psum", bufs=1))
+        ctx.enter_context(tc.manual_schedule())
+
+        ident = keep.tile([P, P], F32, name="ident")
+        make_identity(nc, ident[:])
+        scale_raw = keep.tile([P, KP, T // 4], I32, name="scale_raw")
+        idf_rows = keep.tile([P, P], BF16, name="idf_rows")
+        warm = keep.tile([P, 2], F32, name="warm")
+        nc.vector.memset(warm[:, 0:1], 1.0)
+        nc.vector.memset(idf_rows[:], 0.0)
+        nc.vector.memset(scale_raw[:], 0)
+        ident_bf = keep.tile([P, P], BF16, name="ident_bf")
+        nc.vector.tensor_copy(out=ident_bf[:], in_=ident[:])
+
+        norm_col = keep.tile([P, DT], BF16, name="norm_col")
+        nc.scalar.dma_start(out=norm_col[:], in_=norm.rearrange("(p j) -> p j", j=DT))
+        for h in range(2):
+            nc.scalar.dma_start(
+                out=idf_rows[8 * h : 8 * h + 8, :].rearrange("a (q r) -> a q r", r=8),
+                in_=idf[1024 * h : 1024 * (h + 1)].rearrange("(q a r) -> a q r", a=8, r=8),
+            )
+        nc.scalar.activation(out=warm[:, 1:2], in_=warm[:, 0:1], func=ACT.Abs_reciprocal_sqrt)
+
+        docs_by_tile = docs.rearrange("(p j) k -> p j k", j=DT)
+        doc_raw = {}
+
+        def load_docs(first, count):
+            raw = keep.tile([P, count, K], BF16, name="doc_raw_%d" % first)
+            nc.sync.dma_start(out=raw[:], in_=docs_by_tile[:, first : first + count, :])
+            for i in range(count):
+                doc_raw[first + i] = raw[:, i, :]
+
+        words = e_words.bitcast(I32)
+        code_raw = []
+
+        def load_codes(h):
+            raw = keep.tile([P, KP, 512], I32, name="code_raw_%d" % h)
+            nc.sync.dma_start(out=raw[:], in_=words[:, :, 512 * h : 512 * (h + 1)].rearrange("k p w -> p k w"))
+            code_raw.append(raw)
+
+        query_raw = []
+
+        def load_queries(h):
+            raw = keep.tile([P, 8, NQ], BF16, name="query_raw_%d" % h)
+            rows = queries[1024 * h : 1024 * (h + 1), :].rearrange("(q a r) n -> r q a n", a=8, r=8)
+            for r in range(8):
+                nc.sync.dma_start(out=raw[r:P:8, :, :], in_=rows[r])
+            query_raw.append(raw)
+
+        load_docs(0, 1)
+        load_docs(1, 1)
+        load_codes(0)
+        scale_rows = e_scales.bitcast(I32)
+        for r in range(4):
+            nc.sync.dma_start(out=scale_raw[r:P:32, :, :], in_=scale_rows[:, r:16:4, :].rearrange("k q w -> q k w"))
+        load_docs(2, 2)
+        load_codes(1)
+        load_queries(0)
+        load_docs(4, 2)
+        load_queries(1)
+        load_docs(6, 2)
+
+        e_codes = {}
+        e_planes = {}
+
+        def sort_codes(g):
+            h, g2 = divmod(g, 2)
+            dst = keep.tile([P, KP, 4, 256], U8, name="e_codes_%d" % g, align_bytes=64)
+            nc.vector.tensor_copy(
+                out=dst[:].bitcast(I32).rearrange("p k t (q r) -> p k t q r", r=4),
+                in_=code_raw[h][:].rearrange("p k (q g t r) -> p g k t q r", g=2, t=4, r=4)[:, g2],
+            )
+            e_codes[g] = dst
+
+        def sort_scales(h):
+            dst = keep.tile([P, KP, 8, P], U8, name="e_plane_%d" % h, align_bytes=64)
+            nc.vector.tensor_copy(
+                out=dst[:].bitcast(I32).rearrange("p k a (q r) -> p k a q r", r=2),
+                in_=scale_raw[:, :, 256 * h : 256 * (h + 1)].rearrange("p k (q a r) -> p k a q r", a=8, r=2),
+            )
+            e_planes[h] = dst
+
+        doc_grouped = {}
+        doc_codes = {}
+        doc_planes = {}
+
+        def turn_docs(j):
+            bank = psum.tile([P, KP, 2, P], F32, name="aux", tag="aux", bufs=2)
+            pairs = doc_raw[j].bitcast(F32)
+            for k in range(KP):
+                for u in range(2):
+                    nc.tensor.transpose(bank[:, k, u, :], pairs[:, 256 * k + u : 256 * (k + 1) : 2], ident[:])
+            return bank
+
+        def group_docs(j, bank):
+            grouped = work.tile([P, KP, P, 2], F32, name="doc_grouped", bufs=2, align_bytes=64)
+            nc.scalar.copy(out=grouped[:], in_=bank[:].rearrange("p k u m -> p k m u"))
+            doc_grouped[j] = grouped
+
+        def quantize_docs(j):
+            codes = keep.tile([P, KP, P], U32, name="doc_codes_%d" % j, align_bytes=64)
+            plane = keep.tile([P, KP, P], U8, name="doc_plane_%d" % j, align_bytes=64)
+            nc.vector.quantize_mx(
+                out=codes[:].rearrange("p k m -> p (k m)").bitcast(E4M3),
+                scales=plane[:].rearrange("p k m -> p (k m)"),
+                in_=doc_grouped[j][:].rearrange("p k m u -> p (k m u)").bitcast(BF16),
+            )
+            doc_codes[j] = codes
+            doc_planes[j] = plane
+
+        query_grouped = {}
+        query_codes = {}
+        query_planes = {}
+
+        def group_queries(g):
+            h, g2 = divmod(g, 2)
+            grouped = keep.tile([P, NQ, 4], BF16, name="query_grouped_%d" % g, align_bytes=64)
+            for n0 in range(0, NQ, 256):
+                nc.gpsimd.tensor_scalar(
+                    out=grouped[:, n0 : n0 + 256, :],
+                    in0=query_raw[h][:, 4 * g2 : 4 * g2 + 4, n0 : n0 + 256].rearrange("p t n -> p n t"),
+                    scalar1=1.0, scalar2=0.0, op0=ALU.mult, op1=ALU.add,
+                )
+            query_grouped[g] = grouped
+
+        def quantize_queries(g):
+            codes = keep.tile([P, NQ], U32, name="query_codes_%d" % g, align_bytes=64)
+            plane = keep.tile([P, NQ], U8, name="query_plane_%d" % g, align_bytes=64)
+            nc.vector.quantize_mx(
+                out=codes[:].bitcast(E4M3), scales=plane[:],
+                in_=query_grouped[g][:].rearrange("p n t -> p (n t)"),
+            )
+            query_codes[g] = codes
+            query_planes[g] = plane
+
+        logits = {}
+        denoms = {}
+        weights = {}
+        impacts = {}
+        impact_codes = {}
+        impact_planes = {}
+
+        def first_product(s):
+            b, g = divmod(s, TP)
+            h, g2 = divmod(g, 2)
+            for i in range(PAIR):
+                j = PAIR * b + i
+                bank = psum.tile([P, 4, P], F32, name="logit", tag="logit", bufs=6)
+                for t in range(4):
+                    for k in range(KP):
+                        nc.tensor.matmul_mx(
+                            out=bank[:, t, :],
+                            lhsT=e_codes[g][:, k, t, :].bitcast(E2M1),
+                            lhsT_scale=e_planes[h][:, k, 4 * g2 + t, :],
+                            rhs=doc_codes[j][:, k, :].bitcast(E4M3),
+                            rhs_scale=doc_planes[j][:, k, :],
+                            start=(k == 0), stop=(k == KP - 1),
+                        )
+                logits[s, i] = bank
+
+        def denominators(s):
+            b = s // TP
+            den = work.tile([P, 4, PAIR * P], F32, name="den")
+            for i in range(PAIR):
+                nc.vector.scalar_tensor_tensor(
+                    out=den[:, :, P * i : P * (i + 1)], in0=logits[s, i][:], scalar=0.0,
+                    in1=norm_rows[:, PAIR * b + i, :].unsqueeze(1).to_broadcast([P, 4, P]),
+                    op0=ALU.max, op1=ALU.add,
+                )
+            denoms[s] = den
+
+        def reciprocals(s):
+            g = s % TP
+            root = work.tile([P, 4, PAIR * P], F32, name="root", bufs=2)
+            for t in range(4):
+                nc.scalar.activation(
+                    out=root[:, t, :], in_=denoms[s][:, t, :], func=ACT.Abs_reciprocal_sqrt,
+                    scale=inv_idf[:, 4 * g + t : 4 * g + t + 1],
+                )
+            for i in range(PAIR):
+                weight = work.tile([P, P, 4], F32, name="weight", bufs=6)
+                nc.scalar.activation(
+                    out=weight[:].rearrange("p (c e) t -> p c t e", e=2),
+                    in_=root[:, :, P * i : P * (i + 1)].rearrange("p t (c e) -> p c t e", e=2),
+                    func=ACT.Square,
+                )
+                weights[s, i] = weight
+
+        def numerators(s):
+            imp = work.tile([P, PAIR, P, 4], BF16, name="impact", align_bytes=64)
+            for i in range(PAIR):
+                nc.vector.scalar_tensor_tensor(
+                    out=imp[:, i], in0=logits[s, i][:].rearrange("p t m -> p m t"), scalar=0.0,
+                    in1=weights[s, i][:], op0=ALU.max, op1=ALU.mult,
+                )
+            impacts[s] = imp
+
+        def quantize_impacts(s, tiles):
+            for lo, hi in tiles:
+                codes = work.tile([P, (hi - lo) * P], U32, name="impact_codes", bufs=9, align_bytes=64)
+                plane = work.tile([P, (hi - lo) * P], U8, name="impact_plane", bufs=9, align_bytes=64)
+                nc.vector.quantize_mx(
+                    out=codes[:].bitcast(E5M2), scales=plane[:],
+                    in_=impacts[s][:, lo:hi].rearrange("p i m t -> p (i m t)"),
+                )
+                for i in range(lo, hi):
+                    impact_codes[s, i] = codes[:, P * (i - lo) : P * (i - lo + 1)]
+                    impact_planes[s, i] = plane[:, P * (i - lo) : P * (i - lo + 1)]
+
+        def second_product(j, bank, passes):
+            b, i = divmod(j, PAIR)
+            for g in passes:
+                nc.tensor.matmul_mx(
+                    out=bank[:],
+                    lhsT=impact_codes[TP * b + g, i].bitcast(E5M2), lhsT_scale=impact_planes[TP * b + g, i],
+                    rhs=query_codes[g][:].bitcast(E4M3), rhs_scale=query_planes[g][:],
+                    start=(g == 0), stop=(g == TP - 1),
+                )
+
+        out_by_tile = out.rearrange("(p j) n -> p j n", j=DT)
+
+        def store_scores(j, bank, on_vector):
+            scores = work.tile([P, NQ], F32, name="scores", bufs=4)
+            if on_vector:
+                nc.vector.tensor_copy(out=scores[:], in_=bank[:])
+            else:
+                nc.scalar.copy(out=scores[:], in_=bank[:])
+            nc.sync.dma_start(out=out_by_tile[:, j, :], in_=scores[:])
+
+        norm_bank = psum.tile([P, DT, P], BF16, name="norm_bank", tag="logit", bufs=6)
+        for j in range(DT):
+            nc.tensor.transpose(norm_bank[:, j, :], norm_col[:, j : j + 1].to_broadcast([P, P]), ident_bf[:])
+        idf_bank = psum.tile([P, P], BF16, name="idf_bank", tag="logit", bufs=6)
+        nc.tensor.transpose(idf_bank[:], idf_rows[:], ident_bf[:])
+        norm_rows = keep.tile([P, DT, P], BF16, name="norm_rows")
+        nc.scalar.copy(out=norm_rows[:], in_=norm_bank[:])
+        inv_idf = keep.tile([P, 4 * TP], F32, name="inv_idf")
+        nc.vector.reciprocal(out=inv_idf[:], in_=idf_bank[:, 0 : 4 * TP])
+        for j in range(PAIR):
+            group_docs(j, turn_docs(j))
+        sort_codes(0)
+        quantize_docs(0)
+        sort_scales(0)
+        quantize_docs(1)
+        sort_codes(1)
+        first_product(0)
+        for g in range(TP):
+            group_queries(g)
+
+        last_banks = {}
+        for s in range(UNITS + 2):
+            b, g = divmod(s, TP)
+            if s >= 2:
+                numerators(s - 2)
+            if s + 1 < UNITS:
+                first_product(s + 1)
+            if s < UNITS:
+                denominators(s)
+                reciprocals(s)
+            if s >= 2:
+                quantize_impacts(s - 2, [(0, 1), (1, 2)] if s == UNITS + 1 else [(0, PAIR)])
+            if s == 0:
+                sort_codes(2)
+                sort_scales(1)
+                sort_codes(3)
+            nxt = PAIR * (b + 1)
+            if nxt < DT and g in (1, 2):
+                quantize_docs(nxt + g - 1)
+            if nxt < DT and g in (0, 1):
+                group_docs(nxt + g, turn_docs(nxt + g))
+            if 2 <= s < 2 + TP:
+                quantize_queries(s - 2)
+            if 1 <= b < DT // PAIR and g in (2, 3):
+                j = PAIR * (b - 1) + g - 2
+                bank = psum.tile([P, NQ], F32, name="aux", tag="aux", bufs=2)
+                second_product(j, bank, range(TP))
+                store_scores(j, bank, False)
+            if s == UNITS:
+                for i in range(PAIR):
+                    last_banks[i] = psum.tile([P, NQ], F32, name="last", tag="logit", bufs=6)
+                    second_product(DT - PAIR + i, last_banks[i], range(TP - 1))
+        for i in range(PAIR):
+            second_product(DT - PAIR + i, last_banks[i], [TP - 1])
+        for i in range(PAIR):
+            store_scores(DT - PAIR + i, last_banks[i], i == 1)

@@ -21,8 +21,13 @@ P = 128
 KP = K // 512
 TP = T // 512
 DT = D // P
-PAIR = 2
-UNITS = (DT // PAIR) * TP
+HT = 4
+W = HT * P
+UNITS = 2 * TP
+STEPS = 4 * UNITS
+LAG = 3
+JOB_STEPS = 3
+PARTS = ((0, 1), (1, 3))
 
 
 def tile_learned_bm25_scores_s9_kernel(tc, docs, e_words, e_scales, norm, idf, queries, out):
@@ -35,22 +40,18 @@ def tile_learned_bm25_scores_s9_kernel(tc, docs, e_words, e_scales, norm, idf, q
 
         ident = keep.tile([P, P], F32, name="ident")
         make_identity(nc, ident[:])
-        scale_raw = keep.tile([P, KP, T // 4], I32, name="scale_raw")
+        scale_raw = [keep.tile([P, KP, P * count], I32, name="scale_raw_%d" % first) for first, count in PARTS]
         idf_rows = keep.tile([P, P], BF16, name="idf_rows")
         warm = keep.tile([P, 2], F32, name="warm")
+        nc.vector.memset(scale_raw[0][:], 0)
         nc.vector.memset(warm[:, 0:1], 1.0)
         nc.vector.memset(idf_rows[:], 0.0)
-        nc.vector.memset(scale_raw[:], 0)
+        nc.vector.memset(scale_raw[1][:], 0)
         ident_bf = keep.tile([P, P], BF16, name="ident_bf")
         nc.vector.tensor_copy(out=ident_bf[:], in_=ident[:])
 
         norm_col = keep.tile([P, DT], BF16, name="norm_col")
         nc.scalar.dma_start(out=norm_col[:], in_=norm.rearrange("(p j) -> p j", j=DT))
-        for h in range(2):
-            nc.scalar.dma_start(
-                out=idf_rows[8 * h : 8 * h + 8, :].rearrange("a (q r) -> a q r", r=8),
-                in_=idf[1024 * h : 1024 * (h + 1)].rearrange("(q a r) -> a q r", a=8, r=8),
-            )
         nc.scalar.activation(out=warm[:, 1:2], in_=warm[:, 0:1], func=ACT.Abs_reciprocal_sqrt)
 
         docs_by_tile = docs.rearrange("(p j) k -> p j k", j=DT)
@@ -63,30 +64,49 @@ def tile_learned_bm25_scores_s9_kernel(tc, docs, e_words, e_scales, norm, idf, q
                 doc_raw[first + i] = raw[:, i, :]
 
         words = e_words.bitcast(I32)
-        code_raw = []
+        scale_rows = e_scales.bitcast(I32)
+        code_raw = {}
+        query_raw = {}
 
         def load_codes(h):
-            raw = keep.tile([P, KP, 512], I32, name="code_raw_%d" % h)
-            nc.sync.dma_start(out=raw[:], in_=words[:, :, 512 * h : 512 * (h + 1)].rearrange("k p w -> p k w"))
-            code_raw.append(raw)
+            first, count = PARTS[h]
+            raw = keep.tile([P, KP, 256 * count], I32, name="code_raw_%d" % h)
+            nc.sync.dma_start(out=raw[:], in_=words[:, :, 256 * first : 256 * (first + count)].rearrange("k p w -> p k w"))
+            code_raw[h] = raw
 
-        query_raw = []
+        def load_scales(h):
+            first, count = PARTS[h]
+            for r in range(4):
+                nc.sync.dma_start(
+                    out=scale_raw[h][r:P:32, :, :],
+                    in_=scale_rows[:, r:16:4, P * first : P * (first + count)].rearrange("k q w -> q k w"),
+                )
+
+        def load_idf(h):
+            first, count = PARTS[h]
+            nc.sync.dma_start(
+                out=idf_rows[4 * first : 4 * (first + count), :].rearrange("a (q r) -> a q r", r=8),
+                in_=idf[512 * first : 512 * (first + count)].rearrange("(q a r) -> a q r", q=16, r=8),
+            )
 
         def load_queries(h):
-            raw = keep.tile([P, 8, NQ], BF16, name="query_raw_%d" % h)
-            rows = queries[1024 * h : 1024 * (h + 1), :].rearrange("(q a r) n -> r q a n", a=8, r=8)
+            first, count = PARTS[h]
+            raw = keep.tile([P, 4 * count, NQ], BF16, name="query_raw_%d" % h)
+            rows = queries[512 * first : 512 * (first + count), :].rearrange("(q a r) n -> r q a n", q=16, r=8)
             for r in range(8):
                 nc.sync.dma_start(out=raw[r:P:8, :, :], in_=rows[r])
-            query_raw.append(raw)
+            for g in range(count):
+                query_raw[first + g] = raw[:, 4 * g : 4 * g + 4, :]
 
         load_docs(0, 1)
-        load_docs(1, 1)
         load_codes(0)
-        scale_rows = e_scales.bitcast(I32)
-        for r in range(4):
-            nc.sync.dma_start(out=scale_raw[r:P:32, :, :], in_=scale_rows[:, r:16:4, :].rearrange("k q w -> q k w"))
+        load_docs(1, 1)
+        load_scales(0)
         load_docs(2, 2)
+        load_idf(0)
+        load_idf(1)
         load_codes(1)
+        load_scales(1)
         load_queries(0)
         load_docs(4, 2)
         load_queries(1)
@@ -96,156 +116,170 @@ def tile_learned_bm25_scores_s9_kernel(tc, docs, e_words, e_scales, norm, idf, q
         e_planes = {}
 
         def sort_codes(g):
-            h, g2 = divmod(g, 2)
+            h = min(g, 1)
+            first, count = PARTS[h]
             dst = keep.tile([P, KP, 4, 256], U8, name="e_codes_%d" % g, align_bytes=64)
             nc.vector.tensor_copy(
                 out=dst[:].bitcast(I32).rearrange("p k t (q r) -> p k t q r", r=4),
-                in_=code_raw[h][:].rearrange("p k (q g t r) -> p g k t q r", g=2, t=4, r=4)[:, g2],
+                in_=code_raw[h][:].rearrange("p k (q g t r) -> p g k t q r", g=count, t=4, r=4)[:, g - first],
             )
             e_codes[g] = dst
 
         def sort_scales(h):
-            dst = keep.tile([P, KP, 8, P], U8, name="e_plane_%d" % h, align_bytes=64)
+            first, count = PARTS[h]
+            dst = keep.tile([P, KP, 4 * count, P], U8, name="e_plane_%d" % h, align_bytes=64)
             nc.vector.tensor_copy(
                 out=dst[:].bitcast(I32).rearrange("p k a (q r) -> p k a q r", r=2),
-                in_=scale_raw[:, :, 256 * h : 256 * (h + 1)].rearrange("p k (q a r) -> p k a q r", a=8, r=2),
+                in_=scale_raw[h][:].rearrange("p k (q a r) -> p k a q r", q=16, r=2),
             )
-            e_planes[h] = dst
+            for g in range(count):
+                e_planes[first + g] = dst[:, :, 4 * g : 4 * g + 4, :]
 
+        late_grouped = keep.tile([P, KP, W, 2], F32, name="late_grouped", align_bytes=64)
         doc_grouped = {}
-        doc_codes = {}
-        doc_planes = {}
+        doc_codes = [keep.tile([P, KP, W], U32, name="doc_codes_%d" % a, align_bytes=64) for a in range(2)]
+        doc_planes = [keep.tile([P, KP, W], U8, name="doc_plane_%d" % a, align_bytes=64) for a in range(2)]
 
         def turn_docs(j):
-            bank = psum.tile([P, KP, 2, P], F32, name="aux", tag="aux", bufs=2)
+            a, i = divmod(j, HT)
+            bank = psum.tile([P, KP, 2, P], F32, name="turned", tag="aux", bufs=2)
             pairs = doc_raw[j].bitcast(F32)
             for k in range(KP):
                 for u in range(2):
                     nc.tensor.transpose(bank[:, k, u, :], pairs[:, 256 * k + u : 256 * (k + 1) : 2], ident[:])
-            return bank
+            if a == 1:
+                dst = late_grouped[:, :, P * i : P * (i + 1), :]
+            elif i == HT - 1:
+                last_early = work.tile([P, KP, P, 2], F32, name="grouped", bufs=1, align_bytes=64)
+                dst = last_early[:]
+            else:
+                early = keep.tile([P, KP, P, 2], F32, name="early_%d" % i, align_bytes=64)
+                dst = early[:]
+            nc.scalar.copy(out=dst, in_=bank[:].rearrange("p k u m -> p k m u"))
+            doc_grouped[j] = dst
 
-        def group_docs(j, bank):
-            grouped = work.tile([P, KP, P, 2], F32, name="doc_grouped", bufs=2, align_bytes=64)
-            nc.scalar.copy(out=grouped[:], in_=bank[:].rearrange("p k u m -> p k m u"))
-            doc_grouped[j] = grouped
-
-        def quantize_docs(j):
-            codes = keep.tile([P, KP, P], U32, name="doc_codes_%d" % j, align_bytes=64)
-            plane = keep.tile([P, KP, P], U8, name="doc_plane_%d" % j, align_bytes=64)
+        def quantize_docs(a, k, lo, hi, src):
             nc.vector.quantize_mx(
-                out=codes[:].rearrange("p k m -> p (k m)").bitcast(E4M3),
-                scales=plane[:].rearrange("p k m -> p (k m)"),
-                in_=doc_grouped[j][:].rearrange("p k m u -> p (k m u)").bitcast(BF16),
+                out=doc_codes[a][:, k, lo:hi].bitcast(E4M3),
+                scales=doc_planes[a][:, k, lo:hi],
+                in_=src[:, k].rearrange("p m u -> p (m u)").bitcast(BF16),
             )
-            doc_codes[j] = codes
-            doc_planes[j] = plane
 
-        query_grouped = {}
-        query_codes = {}
-        query_planes = {}
-
-        def group_queries(g):
-            h, g2 = divmod(g, 2)
-            grouped = keep.tile([P, NQ, 4], BF16, name="query_grouped_%d" % g, align_bytes=64)
-            for n0 in range(0, NQ, 256):
-                nc.gpsimd.tensor_scalar(
-                    out=grouped[:, n0 : n0 + 256, :],
-                    in0=query_raw[h][:, 4 * g2 : 4 * g2 + 4, n0 : n0 + 256].rearrange("p t n -> p n t"),
-                    scalar1=1.0, scalar2=0.0, op0=ALU.mult, op1=ALU.add,
-                )
-            query_grouped[g] = grouped
-
-        def quantize_queries(g):
-            codes = keep.tile([P, NQ], U32, name="query_codes_%d" % g, align_bytes=64)
-            plane = keep.tile([P, NQ], U8, name="query_plane_%d" % g, align_bytes=64)
-            nc.vector.quantize_mx(
-                out=codes[:].bitcast(E4M3), scales=plane[:],
-                in_=query_grouped[g][:].rearrange("p n t -> p (n t)"),
+        def interleave(slots):
+            width = slots.shape[2]
+            grouped = work.tile([P, width, 4], BF16, name="grouped", bufs=1, align_bytes=64)
+            nc.gpsimd.tensor_scalar(
+                out=grouped[:], in0=slots.rearrange("p t n -> p n t"),
+                scalar1=1.0, scalar2=0.0, op0=ALU.mult, op1=ALU.add,
             )
-            query_codes[g] = codes
-            query_planes[g] = plane
+            return grouped
 
+        def quantize(grouped, fmt, name):
+            width = grouped.shape[1]
+            codes = keep.tile([P, width], U32, name=name + "_codes", align_bytes=64)
+            plane = keep.tile([P, width], U8, name=name + "_plane", align_bytes=64)
+            nc.vector.quantize_mx(out=codes[:].bitcast(fmt), scales=plane[:], in_=grouped[:].rearrange("p n t -> p (n t)"))
+            return codes, plane
+
+        query_mx = {}
+        impact_mx = {}
         logits = {}
         denoms = {}
+        roots = {}
         weights = {}
         impacts = {}
-        impact_codes = {}
-        impact_planes = {}
+
+        def by_tiles(s):
+            return s < 4 or s >= STEPS - 8
+
+        def place(s):
+            if s >= STEPS - 8:
+                return 1, 2 + s % 2, (s - (STEPS - 8)) // 2
+            return s // 16, (s // 4) % 4, s % 4
+
+        def e_pass(bank, g, t, k, a, lo, hi):
+            nc.tensor.matmul_mx(
+                out=bank,
+                lhsT=e_codes[g][:, k, t, :].bitcast(E2M1), lhsT_scale=e_planes[g][:, k, t, :],
+                rhs=doc_codes[a][:, k, lo:hi].bitcast(E4M3), rhs_scale=doc_planes[a][:, k, lo:hi],
+                start=(k == 0), stop=(k == KP - 1),
+            )
 
         def first_product(s):
-            b, g = divmod(s, TP)
-            h, g2 = divmod(g, 2)
-            for i in range(PAIR):
-                j = PAIR * b + i
-                bank = psum.tile([P, 4, P], F32, name="logit", tag="logit", bufs=6)
+            a, g, x = place(s)
+            bank = psum.tile([P, W], F32, name="logit", tag="logit", bufs=6)
+            if by_tiles(s):
                 for t in range(4):
                     for k in range(KP):
-                        nc.tensor.matmul_mx(
-                            out=bank[:, t, :],
-                            lhsT=e_codes[g][:, k, t, :].bitcast(E2M1),
-                            lhsT_scale=e_planes[h][:, k, 4 * g2 + t, :],
-                            rhs=doc_codes[j][:, k, :].bitcast(E4M3),
-                            rhs_scale=doc_planes[j][:, k, :],
-                            start=(k == 0), stop=(k == KP - 1),
-                        )
-                logits[s, i] = bank
+                        e_pass(bank[:, P * t : P * (t + 1)], g, t, k, a, P * x, P * (x + 1))
+            else:
+                for k in range(KP):
+                    e_pass(bank[:], g, x, k, a, 0, W)
+            logits[s] = bank
 
         def denominators(s):
-            b = s // TP
-            den = work.tile([P, 4, PAIR * P], F32, name="den")
-            for i in range(PAIR):
+            a, g, x = place(s)
+            den = work.tile([P, W], F32, name="den")
+            if by_tiles(s):
                 nc.vector.scalar_tensor_tensor(
-                    out=den[:, :, P * i : P * (i + 1)], in0=logits[s, i][:], scalar=0.0,
-                    in1=norm_rows[:, PAIR * b + i, :].unsqueeze(1).to_broadcast([P, 4, P]),
+                    out=den[:].rearrange("p (t m) -> p t m", t=4), in0=logits[s][:].rearrange("p (t m) -> p t m", t=4),
+                    scalar=0.0, in1=norm_rows[:, HT * a + x, :].unsqueeze(1).to_broadcast([P, 4, P]),
+                    op0=ALU.max, op1=ALU.add,
+                )
+            else:
+                nc.vector.scalar_tensor_tensor(
+                    out=den[:], in0=logits[s][:], scalar=0.0,
+                    in1=norm_rows[:, HT * a : HT * (a + 1), :].rearrange("p j m -> p (j m)"),
                     op0=ALU.max, op1=ALU.add,
                 )
             denoms[s] = den
 
-        def reciprocals(s):
-            g = s % TP
-            root = work.tile([P, 4, PAIR * P], F32, name="root", bufs=2)
-            for t in range(4):
+        def inverse_roots(s):
+            a, g, x = place(s)
+            root = work.tile([P, W], F32, name="root")
+            pieces = [(t, P * t, P * (t + 1)) for t in range(4)] if by_tiles(s) else [(x, 0, W)]
+            for t, lo, hi in pieces:
                 nc.scalar.activation(
-                    out=root[:, t, :], in_=denoms[s][:, t, :], func=ACT.Abs_reciprocal_sqrt,
+                    out=root[:, lo:hi], in_=denoms[s][:, lo:hi], func=ACT.Abs_reciprocal_sqrt,
                     scale=inv_idf[:, 4 * g + t : 4 * g + t + 1],
                 )
-            for i in range(PAIR):
-                weight = work.tile([P, P, 4], F32, name="weight", bufs=6)
+            roots[s] = root
+
+        def squares(s):
+            weight = work.tile([P, W], F32, name="weight", bufs=4)
+            if by_tiles(s):
                 nc.scalar.activation(
-                    out=weight[:].rearrange("p (c e) t -> p c t e", e=2),
-                    in_=root[:, :, P * i : P * (i + 1)].rearrange("p t (c e) -> p c t e", e=2),
+                    out=weight[:].rearrange("p (c e t) -> p c t e", e=2, t=4),
+                    in_=roots[s][:].rearrange("p (t c e) -> p c t e", e=2, t=4),
                     func=ACT.Square,
                 )
-                weights[s, i] = weight
+            else:
+                nc.scalar.activation(out=weight[:], in_=roots[s][:], func=ACT.Square)
+            weights[s] = weight
 
         def numerators(s):
-            imp = work.tile([P, PAIR, P, 4], BF16, name="impact", align_bytes=64)
-            for i in range(PAIR):
+            u, x = divmod(s, 4)
+            if by_tiles(s):
+                imp = work.tile([P, P, 4], BF16, name="tile_impact", bufs=4, align_bytes=64)
                 nc.vector.scalar_tensor_tensor(
-                    out=imp[:, i], in0=logits[s, i][:].rearrange("p t m -> p m t"), scalar=0.0,
-                    in1=weights[s, i][:], op0=ALU.max, op1=ALU.mult,
+                    out=imp[:], in0=logits[s][:].rearrange("p (t m) -> p m t", t=4), scalar=0.0,
+                    in1=weights[s][:].rearrange("p (m t) -> p m t", t=4), op0=ALU.max, op1=ALU.mult,
                 )
-            impacts[s] = imp
-
-        def quantize_impacts(s, tiles):
-            for lo, hi in tiles:
-                codes = work.tile([P, (hi - lo) * P], U32, name="impact_codes", bufs=9, align_bytes=64)
-                plane = work.tile([P, (hi - lo) * P], U8, name="impact_plane", bufs=9, align_bytes=64)
-                nc.vector.quantize_mx(
-                    out=codes[:].bitcast(E5M2), scales=plane[:],
-                    in_=impacts[s][:, lo:hi].rearrange("p i m t -> p (i m t)"),
+                impacts[s] = imp
+            else:
+                if x == 0:
+                    impacts[u, "slots"] = work.tile([P, 4, W], BF16, name="impact")
+                nc.vector.scalar_tensor_tensor(
+                    out=impacts[u, "slots"][:, x, :], in0=logits[s][:], scalar=0.0,
+                    in1=weights[s][:], op0=ALU.max, op1=ALU.mult,
                 )
-                for i in range(lo, hi):
-                    impact_codes[s, i] = codes[:, P * (i - lo) : P * (i - lo + 1)]
-                    impact_planes[s, i] = plane[:, P * (i - lo) : P * (i - lo + 1)]
 
         def second_product(j, bank, passes):
-            b, i = divmod(j, PAIR)
             for g in passes:
+                codes, plane = impact_mx[j, g]
                 nc.tensor.matmul_mx(
-                    out=bank[:],
-                    lhsT=impact_codes[TP * b + g, i].bitcast(E5M2), lhsT_scale=impact_planes[TP * b + g, i],
-                    rhs=query_codes[g][:].bitcast(E4M3), rhs_scale=query_planes[g][:],
+                    out=bank[:], lhsT=codes.bitcast(E5M2), lhsT_scale=plane,
+                    rhs=query_mx[g][0][:].bitcast(E4M3), rhs_scale=query_mx[g][1][:],
                     start=(g == 0), stop=(g == TP - 1),
                 )
 
@@ -259,59 +293,121 @@ def tile_learned_bm25_scores_s9_kernel(tc, docs, e_words, e_scales, norm, idf, q
                 nc.scalar.copy(out=scores[:], in_=bank[:])
             nc.sync.dma_start(out=out_by_tile[:, j, :], in_=scores[:])
 
-        norm_bank = psum.tile([P, DT, P], BF16, name="norm_bank", tag="logit", bufs=6)
-        for j in range(DT):
-            nc.tensor.transpose(norm_bank[:, j, :], norm_col[:, j : j + 1].to_broadcast([P, P]), ident_bf[:])
-        idf_bank = psum.tile([P, P], BF16, name="idf_bank", tag="logit", bufs=6)
-        nc.tensor.transpose(idf_bank[:], idf_rows[:], ident_bf[:])
+        jobs = [("query", 0, 2), ("query", 1, 2), ("query", 2, 8), ("impact", 1, 0), ("query", 3, 8)]
+        jobs = jobs + [("impact", u, 0) for u in range(2, UNITS - 2)]
+        job_start = {}
+        job_end = {}
+        free_from = 0
+        for kind, index, ready in jobs:
+            begin = max(free_from, 4 * index + 3 + LAG if kind == "impact" else ready)
+            free_from = begin + JOB_STEPS
+            job_start[begin] = (kind, index)
+            job_end[free_from] = (kind, index)
+        pending = {}
+
+        def start_job(kind, index):
+            if kind == "query":
+                pending[kind, index] = interleave(query_raw[index])
+            else:
+                pending[kind, index] = interleave(impacts[index, "slots"][:])
+
+        def finish_job(kind, index):
+            if kind == "query":
+                query_mx[index] = quantize(pending[kind, index], E4M3, "query_%d" % index)
+            else:
+                a, g = divmod(index, TP)
+                codes, plane = quantize(pending[kind, index], E5M2, "impact_%d" % index)
+                for i in range(HT):
+                    impact_mx[HT * a + i, g] = (codes[:, P * i : P * (i + 1)], plane[:, P * i : P * (i + 1)])
+
+        def quantize_tile(s):
+            a, g, x = place(s)
+            codes, plane = quantize(impacts[s], E5M2, "tile_%d" % s)
+            impact_mx[HT * a + x, g] = (codes[:], plane[:])
+
         norm_rows = keep.tile([P, DT, P], BF16, name="norm_rows")
-        nc.scalar.copy(out=norm_rows[:], in_=norm_bank[:])
+
+        def spread_norm(a, tag, bufs):
+            bank = psum.tile([P, HT, P], BF16, name="norm_bank", tag=tag, bufs=bufs)
+            for i in range(HT):
+                j = HT * a + i
+                nc.tensor.transpose(bank[:, i, :], norm_col[:, j : j + 1].to_broadcast([P, P]), ident_bf[:])
+            nc.scalar.copy(out=norm_rows[:, HT * a : HT * (a + 1), :], in_=bank[:])
+
+        def quantize_doc_tile(j):
+            for k in range(KP):
+                quantize_docs(0, k, P * j, P * (j + 1), doc_grouped[j])
+
+        turn_docs(0)
+        spread_norm(0, "logit", 6)
+        turn_docs(1)
+        sort_codes(0)
+        sort_scales(0)
+        quantize_doc_tile(0)
+        first_product(0)
+        idf_bank = psum.tile([P, P], BF16, name="idf_bank", tag="aux", bufs=2)
+        nc.tensor.transpose(idf_bank[:], idf_rows[:], ident_bf[:])
+        quantize_doc_tile(1)
         inv_idf = keep.tile([P, 4 * TP], F32, name="inv_idf")
         nc.vector.reciprocal(out=inv_idf[:], in_=idf_bank[:, 0 : 4 * TP])
-        for j in range(PAIR):
-            group_docs(j, turn_docs(j))
-        sort_codes(0)
-        quantize_docs(0)
-        sort_scales(0)
-        quantize_docs(1)
-        sort_codes(1)
-        first_product(0)
-        for g in range(TP):
-            group_queries(g)
+        turn_docs(2)
+        first_product(1)
 
-        last_banks = {}
-        for s in range(UNITS + 2):
-            b, g = divmod(s, TP)
-            if s >= 2:
-                numerators(s - 2)
-            if s + 1 < UNITS:
-                first_product(s + 1)
-            if s < UNITS:
+        issued = 2
+        banks = {}
+        PRODUCT_AT = [23,24,25,27,29,31,33]
+        COPY_AT = [24,26,27,29,31,33]
+        for s in range(STEPS + LAG):
+            if s < STEPS:
                 denominators(s)
-                reciprocals(s)
-            if s >= 2:
-                quantize_impacts(s - 2, [(0, 1), (1, 2)] if s == UNITS + 1 else [(0, PAIR)])
+                inverse_roots(s)
             if s == 0:
-                sort_codes(2)
+                turn_docs(3)
+            if 1 <= s <= STEPS:
+                squares(s - 1)
+            if s >= LAG:
+                numerators(s - LAG)
+            if s == 2:
+                spread_norm(1, "aux", 2)
+            if s in (3, 5, 7, 9):
+                turn_docs(HT + (s - 3) // 2)
+            if s - LAG - 1 >= STEPS - 8:
+                quantize_tile(s - LAG - 1)
+            if s < 2:
+                quantize_doc_tile(2 + s)
+            if s == 1:
+                sort_codes(1)
                 sort_scales(1)
+            if s == 5:
+                sort_codes(2)
+            while issued <= min(s + (2 if s == 0 else 3), STEPS - 1):
+                first_product(issued)
+                issued = issued + 1
+            if s == 5:
+                quantize_tile(0)
+                quantize_tile(1)
+            if s == 8:
                 sort_codes(3)
-            nxt = PAIR * (b + 1)
-            if nxt < DT and g in (1, 2):
-                quantize_docs(nxt + g - 1)
-            if nxt < DT and g in (0, 1):
-                group_docs(nxt + g, turn_docs(nxt + g))
-            if 2 <= s < 2 + TP:
-                quantize_queries(s - 2)
-            if 1 <= b < DT // PAIR and g in (2, 3):
-                j = PAIR * (b - 1) + g - 2
-                bank = psum.tile([P, NQ], F32, name="aux", tag="aux", bufs=2)
-                second_product(j, bank, range(TP))
-                store_scores(j, bank, False)
-            if s == UNITS:
-                for i in range(PAIR):
-                    last_banks[i] = psum.tile([P, NQ], F32, name="last", tag="logit", bufs=6)
-                    second_product(DT - PAIR + i, last_banks[i], range(TP - 1))
-        for i in range(PAIR):
-            second_product(DT - PAIR + i, last_banks[i], [TP - 1])
-        for i in range(PAIR):
-            store_scores(DT - PAIR + i, last_banks[i], i == 1)
+                quantize_tile(2)
+                quantize_tile(3)
+            if s == 11:
+                for k in range(KP):
+                    quantize_docs(1, k, 0, W, late_grouped)
+            if s in job_end:
+                finish_job(*job_end[s])
+            if s in job_start:
+                start_job(*job_start[s])
+            if s in COPY_AT:
+                j = COPY_AT.index(s)
+                store_scores(j, banks[j], j in (1,3))
+            if s in PRODUCT_AT:
+                j = PRODUCT_AT.index(s)
+                banks[j] = psum.tile([P, NQ], F32, name="score", tag="aux", bufs=2)
+                second_product(j, banks[j], range(TP))
+        bank = psum.tile([P, NQ], F32, name="score", tag="logit", bufs=6)
+        second_product(DT - 1, bank, range(TP - 1))
+        quantize_tile(STEPS - 1)
+        second_product(DT - 1, bank, [TP - 1])
+        for j in range(len(COPY_AT), DT - 1):
+            store_scores(j, banks[j], j in (1,3))
+        store_scores(DT - 1, bank, 7 in (1,3))

@@ -24,31 +24,27 @@ DT = D // P
 HT = 4
 W = HT * P
 UNITS = 2 * TP
-STEPS = 4 * UNITS
-LAG = 3
-JOB_STEPS = 3
-PARTS = ((0, 1), (1, 3))
+LAST = UNITS - 1
 
 
 def tile_learned_bm25_scores_s9_kernel(tc, docs, e_words, e_scales, norm, idf, queries, out):
     nc = tc.nc
     with ExitStack() as ctx:
         keep = ctx.enter_context(tc.tile_pool(name="keep", bufs=1))
-        work = ctx.enter_context(tc.tile_pool(name="work", bufs=3))
-        psum = ctx.enter_context(tc.psum_pool(name="psum", bufs=1))
+        work = ctx.enter_context(tc.tile_pool(name="work", bufs=2))
+        psum = ctx.enter_context(tc.psum_pool(name="psum", bufs=4))
         ctx.enter_context(tc.manual_schedule())
 
         ident = keep.tile([P, P], F32, name="ident")
         make_identity(nc, ident[:])
-        scale_raw = [keep.tile([P, KP, P * count], I32, name="scale_raw_%d" % first) for first, count in PARTS]
-        idf_rows = keep.tile([P, P], BF16, name="idf_rows")
+        scale_first = keep.tile([P, KP, P], I32, name="scale_first")
+        scale_rest = keep.tile([P, KP, 3 * P], I32, name="scale_rest")
+        idf_rows = keep.tile([P, 4, P], F32, name="idf_rows")
         warm = keep.tile([P, 2], F32, name="warm")
-        nc.vector.memset(scale_raw[0][:], 0)
+        nc.vector.memset(scale_first[:], 0)
         nc.vector.memset(warm[:, 0:1], 1.0)
+        nc.vector.memset(scale_rest[:], 0)
         nc.vector.memset(idf_rows[:], 0.0)
-        nc.vector.memset(scale_raw[1][:], 0)
-        ident_bf = keep.tile([P, P], BF16, name="ident_bf")
-        nc.vector.tensor_copy(out=ident_bf[:], in_=ident[:])
 
         norm_col = keep.tile([P, DT], BF16, name="norm_col")
         nc.scalar.dma_start(out=norm_col[:], in_=norm.rearrange("(p j) -> p j", j=DT))
@@ -68,72 +64,65 @@ def tile_learned_bm25_scores_s9_kernel(tc, docs, e_words, e_scales, norm, idf, q
         code_raw = {}
         query_raw = {}
 
-        def load_codes(h):
-            first, count = PARTS[h]
-            raw = keep.tile([P, KP, 256 * count], I32, name="code_raw_%d" % h)
-            nc.sync.dma_start(out=raw[:], in_=words[:, :, 256 * first : 256 * (first + count)].rearrange("k p w -> p k w"))
-            code_raw[h] = raw
+        def load_codes(first, count):
+            raw = keep.tile([P, KP, count, 256], I32, name="code_raw_%d" % first)
+            nc.sync.dma_start(
+                out=raw[:].rearrange("p k g w -> p k (g w)"),
+                in_=words[:, :, 256 * first : 256 * (first + count)].rearrange("k p w -> p k w"),
+            )
+            for g in range(count):
+                code_raw[first + g] = raw[:, :, g, :]
 
-        def load_scales(h):
-            first, count = PARTS[h]
+        def load_scales(dst, first, count):
             for r in range(4):
                 nc.sync.dma_start(
-                    out=scale_raw[h][r:P:32, :, :],
+                    out=dst[r:P:32, :, :],
                     in_=scale_rows[:, r:16:4, P * first : P * (first + count)].rearrange("k q w -> q k w"),
                 )
 
-        def load_idf(h):
-            first, count = PARTS[h]
-            nc.sync.dma_start(
-                out=idf_rows[4 * first : 4 * (first + count), :].rearrange("a (q r) -> a q r", r=8),
-                in_=idf[512 * first : 512 * (first + count)].rearrange("(q a r) -> a q r", q=16, r=8),
-            )
+        def load_queries(g):
+            raw = keep.tile([P, 4, NQ], BF16, name="query_raw_%d" % g)
+            rows = queries[512 * g : 512 * (g + 1), :].rearrange("(m t r) n -> r m t n", t=4, r=4)
+            for r in range(4):
+                nc.sync.dma_start(out=raw[r:P:4, :, :], in_=rows[r])
+            query_raw[g] = raw
 
-        def load_queries(h):
-            first, count = PARTS[h]
-            raw = keep.tile([P, 4 * count, NQ], BF16, name="query_raw_%d" % h)
-            rows = queries[512 * first : 512 * (first + count), :].rearrange("(q a r) n -> r q a n", q=16, r=8)
-            for r in range(8):
-                nc.sync.dma_start(out=raw[r:P:8, :, :], in_=rows[r])
-            for g in range(count):
-                query_raw[first + g] = raw[:, 4 * g : 4 * g + 4, :]
-
+        idf_raw = keep.tile([TP, 512], BF16, name="idf_raw")
         load_docs(0, 1)
-        load_codes(0)
+        load_codes(0, 1)
         load_docs(1, 1)
-        load_scales(0)
+        load_scales(scale_first, 0, 1)
         load_docs(2, 2)
-        load_idf(0)
-        load_idf(1)
-        load_codes(1)
-        load_scales(1)
+        nc.sync.dma_start(out=idf_raw[:], in_=idf.rearrange("(g w) -> g w", g=TP))
+        load_codes(1, 1)
+        load_scales(scale_rest, 1, 3)
         load_queries(0)
         load_docs(4, 2)
+        load_codes(2, 2)
         load_queries(1)
         load_docs(6, 2)
+        load_queries(2)
+        load_queries(3)
 
         e_codes = {}
         e_planes = {}
 
         def sort_codes(g):
-            h = min(g, 1)
-            first, count = PARTS[h]
             dst = keep.tile([P, KP, 4, 256], U8, name="e_codes_%d" % g, align_bytes=64)
             nc.vector.tensor_copy(
-                out=dst[:].bitcast(I32).rearrange("p k t (q r) -> p k t q r", r=4),
-                in_=code_raw[h][:].rearrange("p k (q g t r) -> p g k t q r", g=count, t=4, r=4)[:, g - first],
+                out=dst[:].bitcast(I32).rearrange("p k t (m r) -> p k t m r", r=2),
+                in_=code_raw[g].rearrange("p k (m t r) -> p k t m r", t=4, r=2),
             )
             e_codes[g] = dst
 
-        def sort_scales(h):
-            first, count = PARTS[h]
-            dst = keep.tile([P, KP, 4 * count, P], U8, name="e_plane_%d" % h, align_bytes=64)
+        def sort_scales(src, first, count):
+            dst = keep.tile([P, KP, count, 4, P], U8, name="e_plane_%d" % first, align_bytes=64)
             nc.vector.tensor_copy(
-                out=dst[:].bitcast(I32).rearrange("p k a (q r) -> p k a q r", r=2),
-                in_=scale_raw[h][:].rearrange("p k (q a r) -> p k a q r", q=16, r=2),
+                out=dst[:].bitcast(I32).rearrange("p k g t m -> p (k g) m t"),
+                in_=src[:].rearrange("p k (g m t) -> p (k g) m t", g=count, t=4),
             )
             for g in range(count):
-                e_planes[first + g] = dst[:, :, 4 * g : 4 * g + 4, :]
+                e_planes[first + g] = dst[:, :, g]
 
         late_grouped = keep.tile([P, KP, W, 2], F32, name="late_grouped", align_bytes=64)
         doc_grouped = {}
@@ -142,7 +131,7 @@ def tile_learned_bm25_scores_s9_kernel(tc, docs, e_words, e_scales, norm, idf, q
 
         def turn_docs(j):
             a, i = divmod(j, HT)
-            bank = psum.tile([P, KP, 2, P], F32, name="turned", tag="aux", bufs=2)
+            bank = psum.tile([P, KP, 2, P], F32, name="turned", tag="aux")
             pairs = doc_raw[j].bitcast(F32)
             for k in range(KP):
                 for u in range(2):
@@ -165,37 +154,41 @@ def tile_learned_bm25_scores_s9_kernel(tc, docs, e_words, e_scales, norm, idf, q
                 in_=src[:, k].rearrange("p m u -> p (m u)").bitcast(BF16),
             )
 
-        def interleave(slots):
-            width = slots.shape[2]
-            grouped = work.tile([P, width, 4], BF16, name="grouped", bufs=1, align_bytes=64)
+        def quantize_doc_tile(j):
+            for k in range(KP):
+                quantize_docs(0, k, P * j, P * (j + 1), doc_grouped[j])
+
+        query_codes = [keep.tile([P, NQ], U32, name="query_codes_%d" % g, align_bytes=64) for g in range(TP)]
+        query_planes = [keep.tile([P, NQ], U8, name="query_plane_%d" % g, align_bytes=64) for g in range(TP)]
+
+        def group_queries(g, lo, hi):
+            grouped = work.tile([P, hi - lo, 4], BF16, name="grouped", bufs=1, align_bytes=64)
             nc.gpsimd.tensor_scalar(
-                out=grouped[:], in0=slots.rearrange("p t n -> p n t"),
+                out=grouped[:], in0=query_raw[g][:, :, lo:hi].rearrange("p t n -> p n t"),
                 scalar1=1.0, scalar2=0.0, op0=ALU.mult, op1=ALU.add,
             )
-            return grouped
+            return g, lo, hi, grouped
 
-        def quantize(grouped, fmt, name):
-            width = grouped.shape[1]
-            codes = keep.tile([P, width], U32, name=name + "_codes", align_bytes=64)
-            plane = keep.tile([P, width], U8, name=name + "_plane", align_bytes=64)
-            nc.vector.quantize_mx(out=codes[:].bitcast(fmt), scales=plane[:], in_=grouped[:].rearrange("p n t -> p (n t)"))
-            return codes, plane
+        def quantize_queries(g, lo, hi, grouped):
+            nc.vector.quantize_mx(
+                out=query_codes[g][:, lo:hi].bitcast(E4M3), scales=query_planes[g][:, lo:hi],
+                in_=grouped[:].rearrange("p n t -> p (n t)"),
+            )
 
-        query_mx = {}
+        last_queries = keep.tile([P, NQ, 4], BF16, name="last_queries", align_bytes=64)
+
+        def group_last_queries(lo, hi):
+            nc.scalar.copy(
+                out=last_queries[:, lo:hi, :].rearrange("p (c e) t -> p c t e", e=4),
+                in_=query_raw[TP - 1][:, :, lo:hi].rearrange("p t (c e) -> p c t e", e=4),
+            )
+
         impact_mx = {}
         logits = {}
-        denoms = {}
+        ratios = {}
         roots = {}
         weights = {}
         impacts = {}
-
-        def by_tiles(s):
-            return s < 4 or s >= STEPS - 8
-
-        def place(s):
-            if s >= STEPS - 8:
-                return 1, 2 + s % 2, (s - (STEPS - 8)) // 2
-            return s // 16, (s // 4) % 4, s % 4
 
         def e_pass(bank, g, t, k, a, lo, hi):
             nc.tensor.matmul_mx(
@@ -205,209 +198,220 @@ def tile_learned_bm25_scores_s9_kernel(tc, docs, e_words, e_scales, norm, idf, q
                 start=(k == 0), stop=(k == KP - 1),
             )
 
-        def first_product(s):
-            a, g, x = place(s)
-            bank = psum.tile([P, W], F32, name="logit", tag="logit", bufs=6)
-            if by_tiles(s):
+        def first_product(u, x):
+            a, g = divmod(u, TP)
+            bank = psum.tile([P, W], F32, name="logit", tag="logit")
+            if u in (0, LAST):
                 for t in range(4):
                     for k in range(KP):
                         e_pass(bank[:, P * t : P * (t + 1)], g, t, k, a, P * x, P * (x + 1))
             else:
                 for k in range(KP):
                     e_pass(bank[:], g, x, k, a, 0, W)
-            logits[s] = bank
+            logits[u, x] = bank
 
-        def denominators(s):
-            a, g, x = place(s)
-            den = work.tile([P, W], F32, name="den")
-            if by_tiles(s):
+        def ratio(u, x):
+            a = u // TP
+            if x == 0:
+                ratios[u] = work.tile([P, 4, W], F32, name="ratio", bufs=4)
+            if u in (0, LAST):
                 nc.vector.scalar_tensor_tensor(
-                    out=den[:].rearrange("p (t m) -> p t m", t=4), in0=logits[s][:].rearrange("p (t m) -> p t m", t=4),
-                    scalar=0.0, in1=norm_rows[:, HT * a + x, :].unsqueeze(1).to_broadcast([P, 4, P]),
-                    op0=ALU.max, op1=ALU.add,
+                    out=ratios[u][:, :, P * x : P * (x + 1)], in0=logits[u, x][:].rearrange("p (t m) -> p t m", t=4),
+                    scalar=0.0, in1=inv_norm[:, HT * a + x, :].unsqueeze(1).to_broadcast([P, 4, P]),
+                    op0=ALU.max, op1=ALU.mult,
                 )
             else:
                 nc.vector.scalar_tensor_tensor(
-                    out=den[:], in0=logits[s][:], scalar=0.0,
-                    in1=norm_rows[:, HT * a : HT * (a + 1), :].rearrange("p j m -> p (j m)"),
-                    op0=ALU.max, op1=ALU.add,
-                )
-            denoms[s] = den
-
-        def inverse_roots(s):
-            a, g, x = place(s)
-            root = work.tile([P, W], F32, name="root")
-            pieces = [(t, P * t, P * (t + 1)) for t in range(4)] if by_tiles(s) else [(x, 0, W)]
-            for t, lo, hi in pieces:
-                nc.scalar.activation(
-                    out=root[:, lo:hi], in_=denoms[s][:, lo:hi], func=ACT.Abs_reciprocal_sqrt,
-                    scale=inv_idf[:, 4 * g + t : 4 * g + t + 1],
-                )
-            roots[s] = root
-
-        def squares(s):
-            weight = work.tile([P, W], F32, name="weight", bufs=4)
-            if by_tiles(s):
-                nc.scalar.activation(
-                    out=weight[:].rearrange("p (c e t) -> p c t e", e=2, t=4),
-                    in_=roots[s][:].rearrange("p (t c e) -> p c t e", e=2, t=4),
-                    func=ACT.Square,
-                )
-            else:
-                nc.scalar.activation(out=weight[:], in_=roots[s][:], func=ACT.Square)
-            weights[s] = weight
-
-        def numerators(s):
-            u, x = divmod(s, 4)
-            if by_tiles(s):
-                imp = work.tile([P, P, 4], BF16, name="tile_impact", bufs=4, align_bytes=64)
-                nc.vector.scalar_tensor_tensor(
-                    out=imp[:], in0=logits[s][:].rearrange("p (t m) -> p m t", t=4), scalar=0.0,
-                    in1=weights[s][:].rearrange("p (m t) -> p m t", t=4), op0=ALU.max, op1=ALU.mult,
-                )
-                impacts[s] = imp
-            else:
-                if x == 0:
-                    impacts[u, "slots"] = work.tile([P, 4, W], BF16, name="impact")
-                nc.vector.scalar_tensor_tensor(
-                    out=impacts[u, "slots"][:, x, :], in0=logits[s][:], scalar=0.0,
-                    in1=weights[s][:], op0=ALU.max, op1=ALU.mult,
+                    out=ratios[u][:, x, :], in0=logits[u, x][:], scalar=0.0,
+                    in1=inv_norm[:, HT * a : HT * (a + 1), :].rearrange("p j m -> p (j m)"),
+                    op0=ALU.max, op1=ALU.mult,
                 )
 
-        def second_product(j, bank, passes):
+        def inverse_root(u, t, lo, hi):
+            g = u % TP
+            if u not in roots:
+                roots[u] = work.tile([P, 4, W], F32, name="root")
+            nc.scalar.activation(
+                out=roots[u][:, t, lo:hi], in_=ratios[u][:, t, lo:hi], func=ACT.Abs_reciprocal_sqrt,
+                scale=inv_idf[:, t, g : g + 1], bias=inv_idf[:, t, g : g + 1],
+            )
+
+        def square(u, t0, t1, lo, hi):
+            if u not in weights:
+                weights[u] = work.tile([P, 4, W], F32, name="weight", bufs=3)
+            nc.scalar.activation(out=weights[u][:, t0:t1, lo:hi], in_=roots[u][:, t0:t1, lo:hi], func=ACT.Square)
+
+        def impact(u, lo, hi):
+            if u not in impacts:
+                impacts[u] = work.tile([P, W, 4], BF16, name="impact", align_bytes=64)
+            nc.vector.tensor_tensor(
+                out=impacts[u][:, lo:hi, :].rearrange("p (c e) t -> p c t e", e=2),
+                in0=ratios[u][:, :, lo:hi].rearrange("p t (c e) -> p c t e", e=2),
+                in1=weights[u][:, :, lo:hi].rearrange("p t (c e) -> p c t e", e=2),
+                op=ALU.mult,
+            )
+
+        def quantize_impact(u, lo, hi):
+            a, g = divmod(u, TP)
+            codes = keep.tile([P, hi - lo], U32, name="impact_codes_%d_%d" % (u, lo), align_bytes=64)
+            plane = keep.tile([P, hi - lo], U8, name="impact_plane_%d_%d" % (u, lo), align_bytes=64)
+            nc.vector.quantize_mx(
+                out=codes[:].bitcast(E5M2), scales=plane[:], in_=impacts[u][:, lo:hi, :].rearrange("p n t -> p (n t)")
+            )
+            for i in range(lo // P, hi // P):
+                impact_mx[HT * a + i, g] = (codes[:, P * i - lo : P * (i + 1) - lo], plane[:, P * i - lo : P * (i + 1) - lo])
+
+        score_banks = {}
+
+        def second_product(j, passes):
+            if j not in score_banks:
+                score_banks[j] = psum.tile([P, NQ], F32, name="score", tag="aux" if j < HT else "logit")
             for g in passes:
                 codes, plane = impact_mx[j, g]
                 nc.tensor.matmul_mx(
-                    out=bank[:], lhsT=codes.bitcast(E5M2), lhsT_scale=plane,
-                    rhs=query_mx[g][0][:].bitcast(E4M3), rhs_scale=query_mx[g][1][:],
+                    out=score_banks[j][:], lhsT=codes.bitcast(E5M2), lhsT_scale=plane,
+                    rhs=query_codes[g][:].bitcast(E4M3), rhs_scale=query_planes[g][:],
                     start=(g == 0), stop=(g == TP - 1),
                 )
 
         out_by_tile = out.rearrange("(p j) n -> p j n", j=DT)
 
-        def store_scores(j, bank, on_vector):
+        def store_scores(j, on_vector):
             scores = work.tile([P, NQ], F32, name="scores", bufs=4)
             if on_vector:
-                nc.vector.tensor_copy(out=scores[:], in_=bank[:])
+                nc.vector.tensor_copy(out=scores[:], in_=score_banks[j][:])
             else:
-                nc.scalar.copy(out=scores[:], in_=bank[:])
+                nc.scalar.copy(out=scores[:], in_=score_banks[j][:])
             nc.sync.dma_start(out=out_by_tile[:, j, :], in_=scores[:])
 
-        jobs = [("query", 0, 2), ("query", 1, 2), ("query", 2, 8), ("impact", 1, 0), ("query", 3, 8)]
-        jobs = jobs + [("impact", u, 0) for u in range(2, UNITS - 2)]
-        job_start = {}
-        job_end = {}
-        free_from = 0
-        for kind, index, ready in jobs:
-            begin = max(free_from, 4 * index + 3 + LAG if kind == "impact" else ready)
-            free_from = begin + JOB_STEPS
-            job_start[begin] = (kind, index)
-            job_end[free_from] = (kind, index)
-        pending = {}
+        inv_norm_col = keep.tile([P, DT], F32, name="inv_norm_col")
+        inv_norm = keep.tile([P, DT, P], F32, name="inv_norm")
 
-        def start_job(kind, index):
-            if kind == "query":
-                pending[kind, index] = interleave(query_raw[index])
-            else:
-                pending[kind, index] = interleave(impacts[index, "slots"][:])
-
-        def finish_job(kind, index):
-            if kind == "query":
-                query_mx[index] = quantize(pending[kind, index], E4M3, "query_%d" % index)
-            else:
-                a, g = divmod(index, TP)
-                codes, plane = quantize(pending[kind, index], E5M2, "impact_%d" % index)
-                for i in range(HT):
-                    impact_mx[HT * a + i, g] = (codes[:, P * i : P * (i + 1)], plane[:, P * i : P * (i + 1)])
-
-        def quantize_tile(s):
-            a, g, x = place(s)
-            codes, plane = quantize(impacts[s], E5M2, "tile_%d" % s)
-            impact_mx[HT * a + x, g] = (codes[:], plane[:])
-
-        norm_rows = keep.tile([P, DT, P], BF16, name="norm_rows")
-
-        def spread_norm(a, tag, bufs):
-            bank = psum.tile([P, HT, P], BF16, name="norm_bank", tag=tag, bufs=bufs)
+        def spread_norm(a):
+            bank = psum.tile([P, HT, P], F32, name="norm_bank", tag="aux")
             for i in range(HT):
                 j = HT * a + i
-                nc.tensor.transpose(bank[:, i, :], norm_col[:, j : j + 1].to_broadcast([P, P]), ident_bf[:])
-            nc.scalar.copy(out=norm_rows[:, HT * a : HT * (a + 1), :], in_=bank[:])
+                nc.tensor.transpose(bank[:, i, :], inv_norm_col[:, j : j + 1].to_broadcast([P, P]), ident[:])
+            nc.scalar.copy(out=inv_norm[:, HT * a : HT * (a + 1), :], in_=bank[:])
 
-        def quantize_doc_tile(j):
-            for k in range(KP):
-                quantize_docs(0, k, P * j, P * (j + 1), doc_grouped[j])
+        inv_idf = keep.tile([P, 4, TP], F32, name="inv_idf")
 
+        def turn_idf():
+            nc.vector.tensor_copy(
+                out=idf_rows[0:TP].rearrange("g t (m r) -> g t m r", r=4),
+                in_=idf_raw[:].rearrange("g (m t r) -> g t m r", t=4, r=4),
+            )
+            bank = psum.tile([P, 4, P], F32, name="idf_bank", tag="aux")
+            for t in range(4):
+                nc.tensor.transpose(bank[:, t, :], idf_rows[:, t, :], ident[:])
+            return bank
+
+        nc.vector.reciprocal(out=inv_norm_col[:], in_=norm_col[:])
         turn_docs(0)
-        spread_norm(0, "logit", 6)
+        spread_norm(0)
         turn_docs(1)
         sort_codes(0)
-        sort_scales(0)
+        sort_scales(scale_first, 0, 1)
         quantize_doc_tile(0)
-        first_product(0)
-        idf_bank = psum.tile([P, P], BF16, name="idf_bank", tag="aux", bufs=2)
-        nc.tensor.transpose(idf_bank[:], idf_rows[:], ident_bf[:])
-        quantize_doc_tile(1)
-        inv_idf = keep.tile([P, 4 * TP], F32, name="inv_idf")
-        nc.vector.reciprocal(out=inv_idf[:], in_=idf_bank[:, 0 : 4 * TP])
+        first_product(0, 0)
         turn_docs(2)
-        first_product(1)
+        quantize_doc_tile(1)
+        first_product(0, 1)
+        turn_docs(3)
+        ratio(0, 0)
+        idf_bank = turn_idf()
+        quantize_doc_tile(2)
+        first_product(0, 2)
+        ratio(0, 1)
+        nc.vector.reciprocal(out=inv_idf[:], in_=idf_bank[:, :, 0:TP])
+        for t in range(4):
+            inverse_root(0, t, 0, W // 2)
+        sort_codes(1)
+        sort_scales(scale_rest, 1, 3)
+        quantize_doc_tile(3)
+        first_product(0, 3)
+        pending = group_queries(0, 0, NQ)
+        ratio(0, 2)
+        first_product(1, 0)
+        first_product(1, 1)
+        square(0, 0, 4, 0, W // 2)
+        ratio(0, 3)
+        first_product(1, 2)
+        first_product(1, 3)
+        for t in range(4):
+            inverse_root(0, t, W // 2, W)
+        turn_docs(HT)
+        square(0, 0, 4, W // 2, W)
 
-        issued = 2
-        banks = {}
-        PRODUCT_AT = [23,24,25,27,29,31,33]
-        COPY_AT = [24,26,27,29,31,33]
-        for s in range(STEPS + LAG):
-            if s < STEPS:
-                denominators(s)
-                inverse_roots(s)
-            if s == 0:
-                turn_docs(3)
-            if 1 <= s <= STEPS:
-                squares(s - 1)
-            if s >= LAG:
-                numerators(s - LAG)
-            if s == 2:
-                spread_norm(1, "aux", 2)
-            if s in (3, 5, 7, 9):
-                turn_docs(HT + (s - 3) // 2)
-            if s - LAG - 1 >= STEPS - 8:
-                quantize_tile(s - LAG - 1)
-            if s < 2:
-                quantize_doc_tile(2 + s)
-            if s == 1:
-                sort_codes(1)
-                sort_scales(1)
-            if s == 5:
-                sort_codes(2)
-            while issued <= min(s + (2 if s == 0 else 3), STEPS - 1):
-                first_product(issued)
-                issued = issued + 1
-            if s == 5:
-                quantize_tile(0)
-                quantize_tile(1)
-            if s == 8:
+        halves = [(g, lo, lo + NQ // 2) for g in (1, 2) for lo in (0, NQ // 2)]
+        for u in range(1, UNITS):
+            for x in range(4):
+                ratio(u, x)
+                if u == 1 and x == 3:
+                    sort_codes(2)
+                if u + 1 < UNITS and not (u == 1 and x < 3):
+                    for y in (range(4) if u == 1 else [x]):
+                        first_product(u + 1, y)
+                if u < LAST:
+                    inverse_root(u, x, 0, W)
+                else:
+                    for t in range(4):
+                        inverse_root(u, t, P * x, P * (x + 1))
+                    if x >= 1:
+                        square(u, 0, 4, P * (x - 1), P * x)
+                if u == 1 and x in (0, 2):
+                    turn_docs(HT + 1 + x // 2)
+                if u == 2 and x == 0:
+                    spread_norm(1)
+                if u == 5:
+                    second_product(x, range(2))
+                if u == 6:
+                    second_product(x, range(2, TP))
+            if u < LAST:
+                square(u, 0, 2, 0, W)
+                if u == 1:
+                    turn_docs(DT - 1)
+                if u in (3, 3 + 1):
+                    group_last_queries(256 * (u - 3), 256 * (u - 3 + 1))
+                square(u, 2, 4, 0, W)
+                if u == 6:
+                    for j in range(HT):
+                        if j not in ():
+                            store_scores(j, False)
+            else:
+                square(u, 0, 4, W - P, W)
+            if u >= 2:
+                for lo in (0, W // 2):
+                    impact(u - 2, lo, lo + W // 2)
+            if u == 1:
                 sort_codes(3)
-                quantize_tile(2)
-                quantize_tile(3)
-            if s == 11:
+            if u >= 2:
+                for lo in (0, W // 2):
+                    quantize_impact(u - 2, lo, lo + W // 2)
+            if u == 2:
                 for k in range(KP):
                     quantize_docs(1, k, 0, W, late_grouped)
-            if s in job_end:
-                finish_job(*job_end[s])
-            if s in job_start:
-                start_job(*job_start[s])
-            if s in COPY_AT:
-                j = COPY_AT.index(s)
-                store_scores(j, banks[j], j in (1,3))
-            if s in PRODUCT_AT:
-                j = PRODUCT_AT.index(s)
-                banks[j] = psum.tile([P, NQ], F32, name="score", tag="aux", bufs=2)
-                second_product(j, banks[j], range(TP))
-        bank = psum.tile([P, NQ], F32, name="score", tag="logit", bufs=6)
-        second_product(DT - 1, bank, range(TP - 1))
-        quantize_tile(STEPS - 1)
-        second_product(DT - 1, bank, [TP - 1])
-        for j in range(len(COPY_AT), DT - 1):
-            store_scores(j, banks[j], j in (1,3))
-        store_scores(DT - 1, bank, 7 in (1,3))
+            if u == 6:
+                for j in ():
+                    store_scores(j, True)
+            if u == 5:
+                quantize_queries(TP - 1, 0, NQ, last_queries)
+            if u <= 5:
+                quantize_queries(*pending)
+            if u <= 4:
+                pending = group_queries(*halves[u - 1])
+        for x in range(HT):
+            second_product(HT + x, range(2))
+        for lo in (0, W // 2):
+            impact(LAST - 1, lo, lo + W // 2)
+        for lo in (0, W // 2):
+            quantize_impact(LAST - 1, lo, lo + W // 2)
+        impact(LAST, 0, P)
+        for x in range(HT):
+            second_product(HT + x, [TP - 2])
+        for x in range(HT):
+            if x + 1 < HT:
+                impact(LAST, P * (x + 1), P * (x + 2))
+            quantize_impact(LAST, P * x, P * (x + 1))
+            second_product(HT + x, [TP - 1])
+            store_scores(HT + x, x in ())

@@ -18,13 +18,22 @@ ALU = mybir.AluOpType
 ACT = mybir.ActivationFunctionType
 
 P = 128
-KP = K // 512
-TP = T // 512
+SLOTS = 4
+PASS = P * SLOTS
+KP = K // PASS
+TP = T // PASS
 DT = D // P
-HT = 4
+HT = DT // 2
 W = HT * P
+CODE_WORDS = PASS // 2
+SCALE_WORDS = PASS // 4
+
 UNITS = 2 * TP
 LAST = UNITS - 1
+LAG = 2
+QUERY_HALVES = ((2, 0), (2, NQ // 2), (3, 0))
+SHARED_UNITS = (6, 7)
+SCALAR_QUERIES = 4
 
 
 def tile_learned_bm25_scores_s9_kernel(tc, docs, e_words, e_scales, norm, idf, queries, out):
@@ -35,23 +44,27 @@ def tile_learned_bm25_scores_s9_kernel(tc, docs, e_words, e_scales, norm, idf, q
         psum = ctx.enter_context(tc.psum_pool(name="psum", bufs=4))
         ctx.enter_context(tc.manual_schedule())
 
+        def gpsimd_tile(shape, dtype):
+            return work.tile(shape, dtype, name="gpsimd_out", bufs=1, align_bytes=64)
+
         ident = keep.tile([P, P], F32, name="ident")
         make_identity(nc, ident[:])
-        scale_first = keep.tile([P, KP, P], I32, name="scale_first")
-        scale_rest = keep.tile([P, KP, 3 * P], I32, name="scale_rest")
-        idf_rows = keep.tile([P, 4, P], F32, name="idf_rows")
-        warm = keep.tile([P, 2], F32, name="warm")
+        scale_first = keep.tile([P, KP, SCALE_WORDS], I32, name="scale_first")
+        scale_rest = keep.tile([P, KP, (TP - 1) * SCALE_WORDS], I32, name="scale_rest")
+        idf_rows = keep.tile([P, SLOTS, P], F32, name="idf_rows")
         nc.vector.memset(scale_first[:], 0)
-        nc.vector.memset(warm[:, 0:1], 1.0)
         nc.vector.memset(scale_rest[:], 0)
         nc.vector.memset(idf_rows[:], 0.0)
 
         norm_col = keep.tile([P, DT], BF16, name="norm_col")
         nc.scalar.dma_start(out=norm_col[:], in_=norm.rearrange("(p j) -> p j", j=DT))
-        nc.scalar.activation(out=warm[:, 1:2], in_=warm[:, 0:1], func=ACT.Abs_reciprocal_sqrt)
 
         docs_by_tile = docs.rearrange("(p j) k -> p j k", j=DT)
+        code_words = e_words.bitcast(I32)
+        scale_words = e_scales.bitcast(I32)
         doc_raw = {}
+        code_raw = {}
+        query_raw = {}
 
         def load_docs(first, count):
             raw = keep.tile([P, count, K], BF16, name="doc_raw_%d" % first)
@@ -59,46 +72,40 @@ def tile_learned_bm25_scores_s9_kernel(tc, docs, e_words, e_scales, norm, idf, q
             for i in range(count):
                 doc_raw[first + i] = raw[:, i, :]
 
-        words = e_words.bitcast(I32)
-        scale_rows = e_scales.bitcast(I32)
-        code_raw = {}
-        query_raw = {}
-
-        def load_codes(first, count):
-            raw = keep.tile([P, KP, count, 256], I32, name="code_raw_%d" % first)
+        def load_codes(raw, first, count):
             nc.sync.dma_start(
                 out=raw[:].rearrange("p k g w -> p k (g w)"),
-                in_=words[:, :, 256 * first : 256 * (first + count)].rearrange("k p w -> p k w"),
+                in_=code_words[:, :, CODE_WORDS * first : CODE_WORDS * (first + count)].rearrange("k p w -> p k w"),
             )
             for g in range(count):
                 code_raw[first + g] = raw[:, :, g, :]
 
-        def load_scales(dst, first, count):
+        def load_scales(raw, first, count):
             for r in range(4):
                 nc.sync.dma_start(
-                    out=dst[r:P:32, :, :],
-                    in_=scale_rows[:, r:16:4, P * first : P * (first + count)].rearrange("k q w -> q k w"),
+                    out=raw[r:P:32, :, :],
+                    in_=scale_words[:, r:16:4, SCALE_WORDS * first : SCALE_WORDS * (first + count)].rearrange("k q w -> q k w"),
                 )
 
         def load_queries(g):
-            raw = keep.tile([P, 4, NQ], BF16, name="query_raw_%d" % g)
-            rows = queries[512 * g : 512 * (g + 1), :].rearrange("(m t r) n -> r m t n", t=4, r=4)
+            raw = keep.tile([P, SLOTS, NQ], BF16, name="query_raw_%d" % g)
+            rows = queries[PASS * g : PASS * (g + 1), :].rearrange("(m t r) n -> r m t n", t=SLOTS, r=4)
             for r in range(4):
                 nc.sync.dma_start(out=raw[r:P:4, :, :], in_=rows[r])
             query_raw[g] = raw
 
-        idf_raw = keep.tile([TP, 512], BF16, name="idf_raw")
         load_docs(0, 1)
-        load_codes(0, 1)
+        load_codes(keep.tile([P, KP, 1, CODE_WORDS], I32, name="code_raw_0"), 0, 1)
         load_docs(1, 1)
         load_scales(scale_first, 0, 1)
         load_docs(2, 2)
+        idf_raw = keep.tile([TP, PASS], BF16, name="idf_raw")
         nc.sync.dma_start(out=idf_raw[:], in_=idf.rearrange("(g w) -> g w", g=TP))
-        load_codes(1, 1)
-        load_scales(scale_rest, 1, 3)
+        load_codes(keep.tile([P, KP, 1, CODE_WORDS], I32, name="code_raw_1"), 1, 1)
+        load_scales(scale_rest, 1, TP - 1)
+        load_codes(gpsimd_tile([P, KP, 2, CODE_WORDS], I32), 2, 2)
         load_queries(0)
         load_docs(4, 2)
-        load_codes(2, 2)
         load_queries(1)
         load_docs(6, 2)
         load_queries(2)
@@ -108,160 +115,200 @@ def tile_learned_bm25_scores_s9_kernel(tc, docs, e_words, e_scales, norm, idf, q
         e_planes = {}
 
         def sort_codes(g):
-            dst = keep.tile([P, KP, 4, 256], U8, name="e_codes_%d" % g, align_bytes=64)
+            codes = keep.tile([P, KP, SLOTS, 2 * P], U8, name="e_codes_%d" % g, align_bytes=64)
             nc.vector.tensor_copy(
-                out=dst[:].bitcast(I32).rearrange("p k t (m r) -> p k t m r", r=2),
-                in_=code_raw[g].rearrange("p k (m t r) -> p k t m r", t=4, r=2),
+                out=codes[:].bitcast(I32).rearrange("p k t (m r) -> p k t m r", r=2),
+                in_=code_raw[g].rearrange("p k (m t r) -> p k t m r", t=SLOTS, r=2),
             )
-            e_codes[g] = dst
+            e_codes[g] = codes
 
-        def sort_scales(src, first, count):
-            dst = keep.tile([P, KP, count, 4, P], U8, name="e_plane_%d" % first, align_bytes=64)
+        def sort_scales(raw, first, count):
+            plane = keep.tile([P, KP, count, SLOTS, P], U8, name="e_plane_%d" % first, align_bytes=64)
             nc.vector.tensor_copy(
-                out=dst[:].bitcast(I32).rearrange("p k g t m -> p (k g) m t"),
-                in_=src[:].rearrange("p k (g m t) -> p (k g) m t", g=count, t=4),
+                out=plane[:].bitcast(I32).rearrange("p k g t m -> p (k g) m t"),
+                in_=raw[:].rearrange("p k (g m t) -> p (k g) m t", g=count, t=SLOTS),
             )
             for g in range(count):
-                e_planes[first + g] = dst[:, :, g]
+                e_planes[first + g] = plane[:, :, g]
 
         late_grouped = keep.tile([P, KP, W, 2], F32, name="late_grouped", align_bytes=64)
-        doc_grouped = {}
+        early_grouped = {}
         doc_codes = [keep.tile([P, KP, W], U32, name="doc_codes_%d" % a, align_bytes=64) for a in range(2)]
         doc_planes = [keep.tile([P, KP, W], U8, name="doc_plane_%d" % a, align_bytes=64) for a in range(2)]
 
         def turn_docs(j):
-            a, i = divmod(j, HT)
             bank = psum.tile([P, KP, 2, P], F32, name="turned", tag="aux")
-            pairs = doc_raw[j].bitcast(F32)
+            pairs = doc_raw[j].bitcast(F32).rearrange("p (k m u) -> p k u m", k=KP, u=2)
+            if 0 < j < HT:
+                in_order = work.tile([P, KP, 2, P], F32, name="in_order")
+                nc.vector.tensor_copy(out=in_order[:], in_=pairs)
+                pairs = in_order[:]
             for k in range(KP):
                 for u in range(2):
-                    nc.tensor.transpose(bank[:, k, u, :], pairs[:, 256 * k + u : 256 * (k + 1) : 2], ident[:])
-            if a == 1:
-                dst = late_grouped[:, :, P * i : P * (i + 1), :]
-            elif i == HT - 1:
-                last_early = work.tile([P, KP, P, 2], F32, name="grouped", bufs=1, align_bytes=64)
-                dst = last_early[:]
+                    nc.tensor.transpose(bank[:, k, u, :], pairs[:, k, u, :], ident[:])
+            if j < HT:
+                early_grouped[j] = keep.tile([P, KP, P, 2], F32, name="early_%d" % j, align_bytes=64)
+                grouped = early_grouped[j][:]
             else:
-                early = keep.tile([P, KP, P, 2], F32, name="early_%d" % i, align_bytes=64)
-                dst = early[:]
-            nc.scalar.copy(out=dst, in_=bank[:].rearrange("p k u m -> p k m u"))
-            doc_grouped[j] = dst
+                grouped = late_grouped[:, :, P * (j - HT) : P * (j - HT + 1), :]
+            nc.scalar.copy(out=grouped, in_=bank[:].rearrange("p k u m -> p k m u"))
 
-        def quantize_docs(a, k, lo, hi, src):
-            nc.vector.quantize_mx(
-                out=doc_codes[a][:, k, lo:hi].bitcast(E4M3),
-                scales=doc_planes[a][:, k, lo:hi],
-                in_=src[:, k].rearrange("p m u -> p (m u)").bitcast(BF16),
-            )
-
-        def quantize_doc_tile(j):
+        def quantize_docs(half, lo, hi, grouped):
             for k in range(KP):
-                quantize_docs(0, k, P * j, P * (j + 1), doc_grouped[j])
+                nc.vector.quantize_mx(
+                    out=doc_codes[half][:, k, lo:hi].bitcast(E4M3),
+                    scales=doc_planes[half][:, k, lo:hi],
+                    in_=grouped[:, k].rearrange("p m u -> p (m u)").bitcast(BF16),
+                )
+
+        def quantize_early_docs(j):
+            quantize_docs(0, P * j, P * (j + 1), early_grouped[j])
 
         query_codes = [keep.tile([P, NQ], U32, name="query_codes_%d" % g, align_bytes=64) for g in range(TP)]
         query_planes = [keep.tile([P, NQ], U8, name="query_plane_%d" % g, align_bytes=64) for g in range(TP)]
 
-        def group_queries(g, lo, hi):
-            grouped = work.tile([P, hi - lo, 4], BF16, name="grouped", bufs=1, align_bytes=64)
+        def group_queries(grouped, g, lo, hi):
             nc.gpsimd.tensor_scalar(
                 out=grouped[:], in0=query_raw[g][:, :, lo:hi].rearrange("p t n -> p n t"),
                 scalar1=1.0, scalar2=0.0, op0=ALU.mult, op1=ALU.add,
             )
-            return g, lo, hi, grouped
+            return grouped, g, lo, hi
 
-        def quantize_queries(g, lo, hi, grouped):
+        def quantize_queries(grouped, g, lo, hi):
             nc.vector.quantize_mx(
                 out=query_codes[g][:, lo:hi].bitcast(E4M3), scales=query_planes[g][:, lo:hi],
                 in_=grouped[:].rearrange("p n t -> p (n t)"),
             )
 
-        last_queries = keep.tile([P, NQ, 4], BF16, name="last_queries", align_bytes=64)
+        inv_norm_col = keep.tile([P, DT], F32, name="inv_norm_col")
+        inv_norm = keep.tile([P, DT, P], F32, name="inv_norm")
+        inv_idf = keep.tile([P, SLOTS, TP], F32, name="inv_idf")
 
-        def group_last_queries(lo, hi):
-            nc.scalar.copy(
-                out=last_queries[:, lo:hi, :].rearrange("p (c e) t -> p c t e", e=4),
-                in_=query_raw[TP - 1][:, :, lo:hi].rearrange("p t (c e) -> p c t e", e=4),
+        def invert_norm():
+            norm_root = keep.tile([P, DT], F32, name="norm_root")
+            guess = keep.tile([P, DT], F32, name="guess")
+            minus_one = keep.tile([P, DT], F32, name="minus_one")
+            nc.scalar.activation(out=norm_root[:], in_=norm_col[:], func=ACT.Abs_reciprocal_sqrt)
+            nc.scalar.activation(out=guess[:], in_=norm_root[:], func=ACT.Square)
+            nc.vector.scalar_tensor_tensor(
+                out=minus_one[:], in0=guess[:], scalar=-1.0, in1=norm_col[:], op0=ALU.mult, op1=ALU.mult
+            )
+            nc.vector.scalar_tensor_tensor(
+                out=inv_norm_col[:], in0=minus_one[:], scalar=2.0, in1=guess[:], op0=ALU.add, op1=ALU.mult
             )
 
-        impact_mx = {}
+        def spread_norm(half):
+            bank = psum.tile([P, HT, P], F32, name="norm_bank", tag="aux")
+            for i in range(HT):
+                j = HT * half + i
+                nc.tensor.transpose(bank[:, i, :], inv_norm_col[:, j : j + 1].to_broadcast([P, P]), ident[:])
+            nc.scalar.copy(out=inv_norm[:, HT * half : HT * (half + 1), :], in_=bank[:])
+
+        def turn_idf():
+            nc.vector.tensor_copy(
+                out=idf_rows[0:TP].rearrange("g t (m r) -> g t m r", r=4),
+                in_=idf_raw[:].rearrange("g (m t r) -> g t m r", t=SLOTS, r=4),
+            )
+            bank = psum.tile([P, SLOTS, P], F32, name="idf_bank", tag="aux")
+            for t in range(SLOTS):
+                nc.tensor.transpose(bank[:, t, :], idf_rows[:, t, :], ident[:])
+            return bank
+
         logits = {}
         ratios = {}
         roots = {}
         weights = {}
         impacts = {}
+        impact_mx = {}
+        score_banks = {}
 
-        def e_pass(bank, g, t, k, a, lo, hi):
-            nc.tensor.matmul_mx(
-                out=bank,
-                lhsT=e_codes[g][:, k, t, :].bitcast(E2M1), lhsT_scale=e_planes[g][:, k, t, :],
-                rhs=doc_codes[a][:, k, lo:hi].bitcast(E4M3), rhs_scale=doc_planes[a][:, k, lo:hi],
-                start=(k == 0), stop=(k == KP - 1),
-            )
+        def by_tiles(unit):
+            return unit in (0, LAST)
 
-        def first_product(u, x):
-            a, g = divmod(u, TP)
+        def e_passes(bank, unit, t, lo, hi):
+            half, g = divmod(unit, TP)
+            for k in range(KP):
+                nc.tensor.matmul_mx(
+                    out=bank,
+                    lhsT=e_codes[g][:, k, t, :].bitcast(E2M1), lhsT_scale=e_planes[g][:, k, t, :],
+                    rhs=doc_codes[half][:, k, lo:hi].bitcast(E4M3), rhs_scale=doc_planes[half][:, k, lo:hi],
+                    start=(k == 0), stop=(k == KP - 1),
+                )
+
+        def first_product(unit, x):
             bank = psum.tile([P, W], F32, name="logit", tag="logit")
-            if u in (0, LAST):
-                for t in range(4):
-                    for k in range(KP):
-                        e_pass(bank[:, P * t : P * (t + 1)], g, t, k, a, P * x, P * (x + 1))
+            if by_tiles(unit):
+                for t in range(SLOTS):
+                    e_passes(bank[:, P * t : P * (t + 1)], unit, t, P * x, P * (x + 1))
             else:
-                for k in range(KP):
-                    e_pass(bank[:], g, x, k, a, 0, W)
-            logits[u, x] = bank
+                e_passes(bank[:], unit, x, 0, W)
+            logits[unit, x] = bank
 
-        def ratio(u, x):
-            a = u // TP
+        def ratio(unit, x):
+            half = unit // TP
             if x == 0:
-                ratios[u] = work.tile([P, 4, W], F32, name="ratio", bufs=4)
-            if u in (0, LAST):
+                ratios[unit] = work.tile([P, SLOTS, W], F32, name="ratio", bufs=LAG + 2)
+            if by_tiles(unit):
                 nc.vector.scalar_tensor_tensor(
-                    out=ratios[u][:, :, P * x : P * (x + 1)], in0=logits[u, x][:].rearrange("p (t m) -> p t m", t=4),
-                    scalar=0.0, in1=inv_norm[:, HT * a + x, :].unsqueeze(1).to_broadcast([P, 4, P]),
+                    out=ratios[unit][:, :, P * x : P * (x + 1)],
+                    in0=logits[unit, x][:].rearrange("p (t m) -> p t m", t=SLOTS), scalar=0.0,
+                    in1=inv_norm[:, HT * half + x, :].unsqueeze(1).to_broadcast([P, SLOTS, P]),
                     op0=ALU.max, op1=ALU.mult,
                 )
             else:
                 nc.vector.scalar_tensor_tensor(
-                    out=ratios[u][:, x, :], in0=logits[u, x][:], scalar=0.0,
-                    in1=inv_norm[:, HT * a : HT * (a + 1), :].rearrange("p j m -> p (j m)"),
+                    out=ratios[unit][:, x, :], in0=logits[unit, x][:], scalar=0.0,
+                    in1=inv_norm[:, HT * half : HT * (half + 1), :].rearrange("p j m -> p (j m)"),
                     op0=ALU.max, op1=ALU.mult,
                 )
 
-        def inverse_root(u, t, lo, hi):
-            g = u % TP
-            if u not in roots:
-                roots[u] = work.tile([P, 4, W], F32, name="root")
+        def inverse_root(unit, t, lo, hi):
+            g = unit % TP
+            if unit not in roots:
+                roots[unit] = work.tile([P, SLOTS, W], F32, name="root")
             nc.scalar.activation(
-                out=roots[u][:, t, lo:hi], in_=ratios[u][:, t, lo:hi], func=ACT.Abs_reciprocal_sqrt,
+                out=roots[unit][:, t, lo:hi], in_=ratios[unit][:, t, lo:hi], func=ACT.Abs_reciprocal_sqrt,
                 scale=inv_idf[:, t, g : g + 1], bias=inv_idf[:, t, g : g + 1],
             )
 
-        def square(u, t0, t1, lo, hi):
-            if u not in weights:
-                weights[u] = work.tile([P, 4, W], F32, name="weight", bufs=3)
-            nc.scalar.activation(out=weights[u][:, t0:t1, lo:hi], in_=roots[u][:, t0:t1, lo:hi], func=ACT.Square)
+        def square(unit, t0, t1, lo, hi):
+            if unit not in weights:
+                weights[unit] = work.tile([P, SLOTS, W], F32, name="weight", bufs=LAG + 1)
+            nc.scalar.activation(out=weights[unit][:, t0:t1, lo:hi], in_=roots[unit][:, t0:t1, lo:hi], func=ACT.Square)
 
-        def impact(u, lo, hi):
-            if u not in impacts:
-                impacts[u] = work.tile([P, W, 4], BF16, name="impact", align_bytes=64)
+        def impact(unit, lo, hi):
+            if unit not in impacts:
+                impacts[unit] = work.tile([P, W, SLOTS], BF16, name="impact", align_bytes=64)
             nc.vector.tensor_tensor(
-                out=impacts[u][:, lo:hi, :].rearrange("p (c e) t -> p c t e", e=2),
-                in0=ratios[u][:, :, lo:hi].rearrange("p t (c e) -> p c t e", e=2),
-                in1=weights[u][:, :, lo:hi].rearrange("p t (c e) -> p c t e", e=2),
+                out=impacts[unit][:, lo:hi, :].rearrange("p (c e) t -> p c t e", e=2),
+                in0=ratios[unit][:, :, lo:hi].rearrange("p t (c e) -> p c t e", e=2),
+                in1=weights[unit][:, :, lo:hi].rearrange("p t (c e) -> p c t e", e=2),
                 op=ALU.mult,
             )
 
-        def quantize_impact(u, lo, hi):
-            a, g = divmod(u, TP)
-            codes = keep.tile([P, hi - lo], U32, name="impact_codes_%d_%d" % (u, lo), align_bytes=64)
-            plane = keep.tile([P, hi - lo], U8, name="impact_plane_%d_%d" % (u, lo), align_bytes=64)
-            nc.vector.quantize_mx(
-                out=codes[:].bitcast(E5M2), scales=plane[:], in_=impacts[u][:, lo:hi, :].rearrange("p n t -> p (n t)")
+        def impact_on_gpsimd(unit):
+            piece = gpsimd_tile([P, P, SLOTS], BF16)
+            nc.gpsimd.tensor_tensor(
+                out=piece[:], in0=ratios[unit][:, :, 0:P].rearrange("p t n -> p n t"),
+                in1=weights[unit][:, :, 0:P].rearrange("p t n -> p n t"), op=ALU.mult,
             )
-            for i in range(lo // P, hi // P):
-                impact_mx[HT * a + i, g] = (codes[:, P * i - lo : P * (i + 1) - lo], plane[:, P * i - lo : P * (i + 1) - lo])
+            return piece
 
-        score_banks = {}
+        def quantize_impact(unit, lo, hi, grouped):
+            half, g = divmod(unit, TP)
+            codes = keep.tile([P, hi - lo], U32, name="impact_codes_%d_%d" % (unit, lo), align_bytes=64)
+            plane = keep.tile([P, hi - lo], U8, name="impact_plane_%d_%d" % (unit, lo), align_bytes=64)
+            nc.vector.quantize_mx(out=codes[:].bitcast(E5M2), scales=plane[:], in_=grouped.rearrange("p n t -> p (n t)"))
+            for first in range(lo, hi, P):
+                cols = slice(first - lo, first - lo + P)
+                impact_mx[HT * half + first // P, g] = (codes[:, cols], plane[:, cols])
+
+        def finish_impacts(unit, first):
+            pieces = ((first, W // 2), (W // 2, W))
+            for lo, hi in pieces:
+                impact(unit, lo, hi)
+            for lo, hi in pieces:
+                quantize_impact(unit, lo, hi, impacts[unit][:, lo:hi, :])
 
         def second_product(j, passes):
             if j not in score_banks:
@@ -276,142 +323,112 @@ def tile_learned_bm25_scores_s9_kernel(tc, docs, e_words, e_scales, norm, idf, q
 
         out_by_tile = out.rearrange("(p j) n -> p j n", j=DT)
 
-        def store_scores(j, on_vector):
-            scores = work.tile([P, NQ], F32, name="scores", bufs=4)
-            if on_vector:
-                nc.vector.tensor_copy(out=scores[:], in_=score_banks[j][:])
-            else:
-                nc.scalar.copy(out=scores[:], in_=score_banks[j][:])
+        def store_scores(j):
+            scores = work.tile([P, NQ], F32, name="scores", bufs=HT)
+            nc.scalar.copy(out=scores[:], in_=score_banks[j][:])
             nc.sync.dma_start(out=out_by_tile[:, j, :], in_=scores[:])
 
-        inv_norm_col = keep.tile([P, DT], F32, name="inv_norm_col")
-        inv_norm = keep.tile([P, DT, P], F32, name="inv_norm")
-
-        def spread_norm(a):
-            bank = psum.tile([P, HT, P], F32, name="norm_bank", tag="aux")
-            for i in range(HT):
-                j = HT * a + i
-                nc.tensor.transpose(bank[:, i, :], inv_norm_col[:, j : j + 1].to_broadcast([P, P]), ident[:])
-            nc.scalar.copy(out=inv_norm[:, HT * a : HT * (a + 1), :], in_=bank[:])
-
-        inv_idf = keep.tile([P, 4, TP], F32, name="inv_idf")
-
-        def turn_idf():
-            nc.vector.tensor_copy(
-                out=idf_rows[0:TP].rearrange("g t (m r) -> g t m r", r=4),
-                in_=idf_raw[:].rearrange("g (m t r) -> g t m r", t=4, r=4),
-            )
-            bank = psum.tile([P, 4, P], F32, name="idf_bank", tag="aux")
-            for t in range(4):
-                nc.tensor.transpose(bank[:, t, :], idf_rows[:, t, :], ident[:])
-            return bank
-
-        nc.vector.reciprocal(out=inv_norm_col[:], in_=norm_col[:])
+        invert_norm()
         turn_docs(0)
         spread_norm(0)
-        turn_docs(1)
         sort_codes(0)
+        turn_docs(1)
         sort_scales(scale_first, 0, 1)
-        quantize_doc_tile(0)
+        quantize_early_docs(0)
         first_product(0, 0)
         turn_docs(2)
-        quantize_doc_tile(1)
+        quantize_early_docs(1)
         first_product(0, 1)
         turn_docs(3)
         ratio(0, 0)
         idf_bank = turn_idf()
-        quantize_doc_tile(2)
+        sort_codes(1)
+        quantize_early_docs(2)
         first_product(0, 2)
         ratio(0, 1)
         nc.vector.reciprocal(out=inv_idf[:], in_=idf_bank[:, :, 0:TP])
-        for t in range(4):
+        for t in range(SLOTS):
             inverse_root(0, t, 0, W // 2)
-        sort_codes(1)
-        sort_scales(scale_rest, 1, 3)
-        quantize_doc_tile(3)
+        quantize_early_docs(3)
         first_product(0, 3)
-        pending = group_queries(0, 0, NQ)
+        sort_scales(scale_rest, 1, TP - 1)
+        sort_codes(2)
+        sort_codes(3)
+        queries_0 = group_queries(gpsimd_tile([P, NQ, SLOTS], BF16), 0, 0, NQ)
+        queries_1 = group_queries(keep.tile([P, NQ, SLOTS], BF16, name="queries_1", align_bytes=64), 1, 0, NQ)
         ratio(0, 2)
         first_product(1, 0)
         first_product(1, 1)
-        square(0, 0, 4, 0, W // 2)
+        square(0, 0, SLOTS, 0, W // 2)
         ratio(0, 3)
         first_product(1, 2)
         first_product(1, 3)
-        for t in range(4):
+        for t in range(SLOTS):
             inverse_root(0, t, W // 2, W)
-        turn_docs(HT)
-        square(0, 0, 4, W // 2, W)
+        square(0, 0, SLOTS, W // 2, W)
 
-        halves = [(g, lo, lo + NQ // 2) for g in (1, 2) for lo in (0, NQ // 2)]
-        for u in range(1, UNITS):
-            for x in range(4):
-                ratio(u, x)
-                if u == 1 and x == 3:
-                    sort_codes(2)
-                if u + 1 < UNITS and not (u == 1 and x < 3):
-                    for y in (range(4) if u == 1 else [x]):
-                        first_product(u + 1, y)
-                if u < LAST:
-                    inverse_root(u, x, 0, W)
+        for unit in range(1, UNITS):
+            for x in range(SLOTS):
+                ratio(unit, x)
+                if unit < LAST:
+                    first_product(unit + 1, x)
+                    inverse_root(unit, x, 0, W)
                 else:
-                    for t in range(4):
-                        inverse_root(u, t, P * x, P * (x + 1))
-                    if x >= 1:
-                        square(u, 0, 4, P * (x - 1), P * x)
-                if u == 1 and x in (0, 2):
-                    turn_docs(HT + 1 + x // 2)
-                if u == 2 and x == 0:
-                    spread_norm(1)
-                if u == 5:
-                    second_product(x, range(2))
-                if u == 6:
+                    for t in range(SLOTS):
+                        inverse_root(unit, t, P * x, P * (x + 1))
+                    if x > 0:
+                        square(unit, 0, SLOTS, P * (x - 1), P * x)
+                if unit == TP + 1:
+                    second_product(x, range(0, 2))
+                if unit == TP + 2:
                     second_product(x, range(2, TP))
-            if u < LAST:
-                square(u, 0, 2, 0, W)
-                if u == 1:
-                    turn_docs(DT - 1)
-                if u in (3, 3 + 1):
-                    group_last_queries(256 * (u - 3), 256 * (u - 3 + 1))
-                square(u, 2, 4, 0, W)
-                if u == 6:
-                    for j in range(HT):
-                        if j not in ():
-                            store_scores(j, False)
+            if unit < LAST:
+                square(unit, 0, 2, 0, W)
+                if unit == 1:
+                    for j in range(HT, DT):
+                        turn_docs(j)
+                if unit == 2:
+                    spread_norm(1)
+                if unit == SCALAR_QUERIES:
+                    last_queries = keep.tile([P, NQ // 2, SLOTS], BF16, name="last_queries", align_bytes=64)
+                    nc.scalar.copy(
+                        out=last_queries[:].rearrange("p (c e) t -> p c t e", e=4),
+                        in_=query_raw[TP - 1][:, :, NQ // 2 : NQ].rearrange("p t (c e) -> p c t e", e=4),
+                    )
+                square(unit, 2, SLOTS, 0, W)
             else:
-                square(u, 0, 4, W - P, W)
-            if u >= 2:
-                for lo in (0, W // 2):
-                    impact(u - 2, lo, lo + W // 2)
-            if u == 1:
-                sort_codes(3)
-            if u >= 2:
-                for lo in (0, W // 2):
-                    quantize_impact(u - 2, lo, lo + W // 2)
-            if u == 2:
-                for k in range(KP):
-                    quantize_docs(1, k, 0, W, late_grouped)
-            if u == 6:
-                for j in ():
-                    store_scores(j, True)
-            if u == 5:
-                quantize_queries(TP - 1, 0, NQ, last_queries)
-            if u <= 5:
-                quantize_queries(*pending)
-            if u <= 4:
-                pending = group_queries(*halves[u - 1])
-        for x in range(HT):
-            second_product(HT + x, range(2))
-        for lo in (0, W // 2):
-            impact(LAST - 1, lo, lo + W // 2)
-        for lo in (0, W // 2):
-            quantize_impact(LAST - 1, lo, lo + W // 2)
+                square(unit, 0, SLOTS, W - P, W)
+            if unit == TP + 2:
+                for j in range(HT):
+                    store_scores(j)
+
+            if unit >= LAG:
+                finish_impacts(unit - LAG, P if unit in SHARED_UNITS else 0)
+            if unit == LAG:
+                quantize_queries(*queries_1)
+                quantize_docs(1, 0, W, late_grouped)
+                quantize_queries(*queries_0)
+            if unit == SCALAR_QUERIES + 1:
+                quantize_queries(last_queries, TP - 1, NQ // 2, NQ)
+            if LAG < unit <= LAG + len(QUERY_HALVES):
+                quantize_queries(*query_half)
+            if unit in SHARED_UNITS:
+                quantize_impact(unit - LAG, 0, P, piece[:])
+            if LAG <= unit < LAG + len(QUERY_HALVES):
+                g, lo = QUERY_HALVES[unit - LAG]
+                query_half = group_queries(gpsimd_tile([P, NQ // 2, SLOTS], BF16), g, lo, lo + NQ // 2)
+            if unit + 1 in SHARED_UNITS:
+                piece = impact_on_gpsimd(unit + 1 - LAG)
+
+        for i in range(HT):
+            second_product(HT + i, range(0, 2))
+        finish_impacts(LAST - 1, 0)
         impact(LAST, 0, P)
-        for x in range(HT):
-            second_product(HT + x, [TP - 2])
-        for x in range(HT):
-            if x + 1 < HT:
-                impact(LAST, P * (x + 1), P * (x + 2))
-            quantize_impact(LAST, P * x, P * (x + 1))
-            second_product(HT + x, [TP - 1])
-            store_scores(HT + x, x in ())
+        for i in range(HT):
+            second_product(HT + i, [TP - 2])
+        for i in range(HT):
+            if i + 1 < HT:
+                impact(LAST, P * (i + 1), P * (i + 2))
+            quantize_impact(LAST, P * i, P * (i + 1), impacts[LAST][:, P * i : P * (i + 1), :])
+            second_product(HT + i, [TP - 1])
+            store_scores(HT + i)

@@ -31,9 +31,7 @@ SCALE_WORDS = PASS // 4
 UNITS = 2 * TP
 LAST = UNITS - 1
 LAG = 2
-QUERY_HALVES = ((2, 0), (2, NQ // 2), (3, 0))
-SHARED_UNITS = (6, 7)
-SCALAR_QUERIES = 4
+QUERY_HALVES = ((2, 0), (2, NQ // 2), (3, 0), (3, NQ // 2))
 
 
 def tile_learned_bm25_scores_s9_kernel(tc, docs, e_words, e_scales, norm, idf, queries, out):
@@ -136,13 +134,21 @@ def tile_learned_bm25_scores_s9_kernel(tc, docs, e_words, e_scales, norm, idf, q
         doc_codes = [keep.tile([P, KP, W], U32, name="doc_codes_%d" % a, align_bytes=64) for a in range(2)]
         doc_planes = [keep.tile([P, KP, W], U8, name="doc_plane_%d" % a, align_bytes=64) for a in range(2)]
 
+        sorted_pairs = {}
+
+        def doc_pairs(j):
+            if j in sorted_pairs:
+                return sorted_pairs[j][:]
+            return doc_raw[j].bitcast(F32).rearrange("p (k m u) -> p k u m", k=KP, u=2)
+
+        def sort_docs(j, copy):
+            in_order = keep.tile([P, KP, 2, P], F32, name="in_order_%d" % j)
+            copy(out=in_order[:], in_=doc_pairs(j))
+            sorted_pairs[j] = in_order
+
         def turn_docs(j):
             bank = psum.tile([P, KP, 2, P], F32, name="turned", tag="aux")
-            pairs = doc_raw[j].bitcast(F32).rearrange("p (k m u) -> p k u m", k=KP, u=2)
-            if 0 < j < HT:
-                in_order = work.tile([P, KP, 2, P], F32, name="in_order")
-                nc.vector.tensor_copy(out=in_order[:], in_=pairs)
-                pairs = in_order[:]
+            pairs = doc_pairs(j)
             for k in range(KP):
                 for u in range(2):
                     nc.tensor.transpose(bank[:, k, u, :], pairs[:, k, u, :], ident[:])
@@ -204,11 +210,13 @@ def tile_learned_bm25_scores_s9_kernel(tc, docs, e_words, e_scales, norm, idf, q
                 nc.tensor.transpose(bank[:, i, :], inv_norm_col[:, j : j + 1].to_broadcast([P, P]), ident[:])
             nc.scalar.copy(out=inv_norm[:, HT * half : HT * (half + 1), :], in_=bank[:])
 
-        def turn_idf():
-            nc.vector.tensor_copy(
+        def sort_idf():
+            nc.scalar.copy(
                 out=idf_rows[0:TP].rearrange("g t (m r) -> g t m r", r=4),
                 in_=idf_raw[:].rearrange("g (m t r) -> g t m r", t=SLOTS, r=4),
             )
+
+        def turn_idf():
             bank = psum.tile([P, SLOTS, P], F32, name="idf_bank", tag="aux")
             for t in range(SLOTS):
                 nc.tensor.transpose(bank[:, t, :], idf_rows[:, t, :], ident[:])
@@ -286,29 +294,22 @@ def tile_learned_bm25_scores_s9_kernel(tc, docs, e_words, e_scales, norm, idf, q
                 op=ALU.mult,
             )
 
-        def impact_on_gpsimd(unit):
-            piece = gpsimd_tile([P, P, SLOTS], BF16)
-            nc.gpsimd.tensor_tensor(
-                out=piece[:], in0=ratios[unit][:, :, 0:P].rearrange("p t n -> p n t"),
-                in1=weights[unit][:, :, 0:P].rearrange("p t n -> p n t"), op=ALU.mult,
-            )
-            return piece
-
-        def quantize_impact(unit, lo, hi, grouped):
+        def quantize_impact(unit, lo, hi):
             half, g = divmod(unit, TP)
             codes = keep.tile([P, hi - lo], U32, name="impact_codes_%d_%d" % (unit, lo), align_bytes=64)
             plane = keep.tile([P, hi - lo], U8, name="impact_plane_%d_%d" % (unit, lo), align_bytes=64)
-            nc.vector.quantize_mx(out=codes[:].bitcast(E5M2), scales=plane[:], in_=grouped.rearrange("p n t -> p (n t)"))
+            nc.vector.quantize_mx(
+                out=codes[:].bitcast(E5M2), scales=plane[:], in_=impacts[unit][:, lo:hi, :].rearrange("p n t -> p (n t)")
+            )
             for first in range(lo, hi, P):
                 cols = slice(first - lo, first - lo + P)
                 impact_mx[HT * half + first // P, g] = (codes[:, cols], plane[:, cols])
 
-        def finish_impacts(unit, first):
-            pieces = ((first, W // 2), (W // 2, W))
-            for lo, hi in pieces:
-                impact(unit, lo, hi)
-            for lo, hi in pieces:
-                quantize_impact(unit, lo, hi, impacts[unit][:, lo:hi, :])
+        def finish_impacts(unit):
+            for lo in (0, W // 2):
+                impact(unit, lo, lo + W // 2)
+            for lo in (0, W // 2):
+                quantize_impact(unit, lo, lo + W // 2)
 
         def second_product(j, passes):
             if j not in score_banks:
@@ -324,7 +325,7 @@ def tile_learned_bm25_scores_s9_kernel(tc, docs, e_words, e_scales, norm, idf, q
         out_by_tile = out.rearrange("(p j) n -> p j n", j=DT)
 
         def store_scores(j):
-            scores = work.tile([P, NQ], F32, name="scores", bufs=HT)
+            scores = work.tile([P, NQ], F32, name="scores", bufs=DT)
             nc.scalar.copy(out=scores[:], in_=score_banks[j][:])
             nc.sync.dma_start(out=out_by_tile[:, j, :], in_=scores[:])
 
@@ -332,17 +333,22 @@ def tile_learned_bm25_scores_s9_kernel(tc, docs, e_words, e_scales, norm, idf, q
         turn_docs(0)
         spread_norm(0)
         sort_codes(0)
+        sort_docs(1, nc.vector.tensor_copy)
         turn_docs(1)
+        sort_idf()
+        sort_docs(3, nc.scalar.copy)
         sort_scales(scale_first, 0, 1)
         quantize_early_docs(0)
         first_product(0, 0)
+        sort_docs(2, nc.vector.tensor_copy)
         turn_docs(2)
         quantize_early_docs(1)
         first_product(0, 1)
         turn_docs(3)
+        sort_codes(1)
         ratio(0, 0)
         idf_bank = turn_idf()
-        sort_codes(1)
+        sort_scales(scale_rest, 1, TP - 1)
         quantize_early_docs(2)
         first_product(0, 2)
         ratio(0, 1)
@@ -351,7 +357,6 @@ def tile_learned_bm25_scores_s9_kernel(tc, docs, e_words, e_scales, norm, idf, q
             inverse_root(0, t, 0, W // 2)
         quantize_early_docs(3)
         first_product(0, 3)
-        sort_scales(scale_rest, 1, TP - 1)
         sort_codes(2)
         sort_codes(3)
         queries_0 = group_queries(gpsimd_tile([P, NQ, SLOTS], BF16), 0, 0, NQ)
@@ -380,55 +385,42 @@ def tile_learned_bm25_scores_s9_kernel(tc, docs, e_words, e_scales, norm, idf, q
                         square(unit, 0, SLOTS, P * (x - 1), P * x)
                 if unit == TP + 1:
                     second_product(x, range(0, 2))
-                if unit == TP + 2:
+                if unit == LAST:
                     second_product(x, range(2, TP))
+            if unit == 1:
+                for j in range(HT, DT):
+                    turn_docs(j)
             if unit < LAST:
                 square(unit, 0, 2, 0, W)
-                if unit == 1:
-                    for j in range(HT, DT):
-                        turn_docs(j)
                 if unit == 2:
                     spread_norm(1)
-                if unit == SCALAR_QUERIES:
-                    last_queries = keep.tile([P, NQ // 2, SLOTS], BF16, name="last_queries", align_bytes=64)
-                    nc.scalar.copy(
-                        out=last_queries[:].rearrange("p (c e) t -> p c t e", e=4),
-                        in_=query_raw[TP - 1][:, :, NQ // 2 : NQ].rearrange("p t (c e) -> p c t e", e=4),
-                    )
                 square(unit, 2, SLOTS, 0, W)
             else:
                 square(unit, 0, SLOTS, W - P, W)
-            if unit == TP + 2:
                 for j in range(HT):
                     store_scores(j)
 
             if unit >= LAG:
-                finish_impacts(unit - LAG, P if unit in SHARED_UNITS else 0)
+                finish_impacts(unit - LAG)
             if unit == LAG:
                 quantize_queries(*queries_1)
                 quantize_docs(1, 0, W, late_grouped)
                 quantize_queries(*queries_0)
-            if unit == SCALAR_QUERIES + 1:
-                quantize_queries(last_queries, TP - 1, NQ // 2, NQ)
             if LAG < unit <= LAG + len(QUERY_HALVES):
                 quantize_queries(*query_half)
-            if unit in SHARED_UNITS:
-                quantize_impact(unit - LAG, 0, P, piece[:])
             if LAG <= unit < LAG + len(QUERY_HALVES):
                 g, lo = QUERY_HALVES[unit - LAG]
                 query_half = group_queries(gpsimd_tile([P, NQ // 2, SLOTS], BF16), g, lo, lo + NQ // 2)
-            if unit + 1 in SHARED_UNITS:
-                piece = impact_on_gpsimd(unit + 1 - LAG)
 
         for i in range(HT):
             second_product(HT + i, range(0, 2))
-        finish_impacts(LAST - 1, 0)
+        finish_impacts(LAST - 1)
         impact(LAST, 0, P)
         for i in range(HT):
             second_product(HT + i, [TP - 2])
         for i in range(HT):
             if i + 1 < HT:
                 impact(LAST, P * (i + 1), P * (i + 2))
-            quantize_impact(LAST, P * i, P * (i + 1), impacts[LAST][:, P * i : P * (i + 1), :])
+            quantize_impact(LAST, P * i, P * (i + 1))
             second_product(HT + i, [TP - 1])
             store_scores(HT + i)

from contextlib import ExitStack

import concourse.mybir as mybir
from concourse.masks import make_identity

D, K, T, NQ = 1024, 1024, 2048, 512
FLOPS = 2 * D * K * T + 2 * D * T * NQ

F32 = mybir.dt.float32
BF16 = mybir.dt.bfloat16
I32 = mybir.dt.int32
U32 = mybir.dt.uint32
U8 = mybir.dt.uint8
E4M3 = mybir.dt.float8_e4m3fn_x4
E5M2 = mybir.dt.float8_e5m2_x4
E2M1 = mybir.dt.float4_e2m1fn_x4
ALU = mybir.AluOpType
ACT = mybir.ActivationFunctionType

P = 128
SLOTS = 4
PASS = P * SLOTS
KP = K // PASS
TP = T // PASS
DT = D // P
HT = DT // 2
W = HT * P
CODE_WORDS = PASS // 2
SCALE_WORDS = PASS // 4

UNITS = 2 * TP
LAST = UNITS - 1
LAG = 2
QUERY_HALVES = ((2, 0), (2, NQ // 2), (3, 0), (3, NQ // 2))


def tile_learned_bm25_scores_s9_kernel(tc, docs, e_words, e_scales, norm, idf, queries, out):
    nc = tc.nc
    with ExitStack() as ctx:
        keep = ctx.enter_context(tc.tile_pool(name="keep", bufs=1))
        work = ctx.enter_context(tc.tile_pool(name="work", bufs=2))
        psum = ctx.enter_context(tc.psum_pool(name="psum", bufs=4))
        ctx.enter_context(tc.manual_schedule())

        def gpsimd_tile(shape, dtype):
            return work.tile(shape, dtype, name="gpsimd_out", bufs=1, align_bytes=64)

        ident = keep.tile([P, P], F32, name="ident")
        make_identity(nc, ident[:])
        scale_first = keep.tile([P, KP, SCALE_WORDS], I32, name="scale_first")
        scale_rest = keep.tile([P, KP, (TP - 1) * SCALE_WORDS], I32, name="scale_rest")
        idf_rows = keep.tile([P, SLOTS, P], F32, name="idf_rows")
        nc.vector.memset(scale_first[:], 0)
        nc.vector.memset(scale_rest[:], 0)
        nc.vector.memset(idf_rows[:], 0.0)

        norm_col = keep.tile([P, DT], BF16, name="norm_col")
        nc.scalar.dma_start(out=norm_col[:], in_=norm.rearrange("(p j) -> p j", j=DT))

        docs_by_tile = docs.rearrange("(p j) k -> p j k", j=DT)
        code_words = e_words.bitcast(I32)
        scale_words = e_scales.bitcast(I32)
        doc_raw = {}
        code_raw = {}
        query_raw = {}

        def load_docs(first, count):
            raw = keep.tile([P, count, K], BF16, name="doc_raw_%d" % first)
            nc.sync.dma_start(out=raw[:], in_=docs_by_tile[:, first : first + count, :])
            for i in range(count):
                doc_raw[first + i] = raw[:, i, :]

        def load_codes(raw, first, count):
            nc.sync.dma_start(
                out=raw[:].rearrange("p k g w -> p k (g w)"),
                in_=code_words[:, :, CODE_WORDS * first : CODE_WORDS * (first + count)].rearrange("k p w -> p k w"),
            )
            for g in range(count):
                code_raw[first + g] = raw[:, :, g, :]

        def load_scales(raw, first, count):
            for r in range(4):
                nc.sync.dma_start(
                    out=raw[r:P:32, :, :],
                    in_=scale_words[:, r:16:4, SCALE_WORDS * first : SCALE_WORDS * (first + count)].rearrange("k q w -> q k w"),
                )

        def load_queries(g):
            raw = keep.tile([P, SLOTS, NQ], BF16, name="query_raw_%d" % g)
            rows = queries[PASS * g : PASS * (g + 1), :].rearrange("(m t r) n -> r m t n", t=SLOTS, r=4)
            for r in range(4):
                nc.sync.dma_start(out=raw[r:P:4, :, :], in_=rows[r])
            query_raw[g] = raw

        load_docs(0, 1)
        load_codes(keep.tile([P, KP, 1, CODE_WORDS], I32, name="code_raw_0"), 0, 1)
        load_docs(1, 1)
        load_scales(scale_first, 0, 1)
        load_docs(2, 2)
        idf_raw = keep.tile([TP, PASS], BF16, name="idf_raw")
        nc.sync.dma_start(out=idf_raw[:], in_=idf.rearrange("(g w) -> g w", g=TP))
        load_codes(keep.tile([P, KP, 1, CODE_WORDS], I32, name="code_raw_1"), 1, 1)
        load_scales(scale_rest, 1, TP - 1)
        load_codes(gpsimd_tile([P, KP, 2, CODE_WORDS], I32), 2, 2)
        load_queries(0)
        load_docs(4, 2)
        load_queries(1)
        load_docs(6, 2)
        load_queries(2)
        load_queries(3)

        e_codes = {}
        e_planes = {}

        def sort_codes(g):
            codes = keep.tile([P, KP, SLOTS, 2 * P], U8, name="e_codes_%d" % g, align_bytes=64)
            nc.vector.tensor_copy(
                out=codes[:].bitcast(I32).rearrange("p k t (m r) -> p k t m r", r=2),
                in_=code_raw[g].rearrange("p k (m t r) -> p k t m r", t=SLOTS, r=2),
            )
            e_codes[g] = codes

        def sort_scales(raw, first, count):
            plane = keep.tile([P, KP, count, SLOTS, P], U8, name="e_plane_%d" % first, align_bytes=64)
            nc.vector.tensor_copy(
                out=plane[:].bitcast(I32).rearrange("p k g t m -> p (k g) m t"),
                in_=raw[:].rearrange("p k (g m t) -> p (k g) m t", g=count, t=SLOTS),
            )
            for g in range(count):
                e_planes[first + g] = plane[:, :, g]

        late_grouped = keep.tile([P, KP, W, 2], F32, name="late_grouped", align_bytes=64)
        early_grouped = {}
        doc_codes = [keep.tile([P, KP, W], U32, name="doc_codes_%d" % a, align_bytes=64) for a in range(2)]
        doc_planes = [keep.tile([P, KP, W], U8, name="doc_plane_%d" % a, align_bytes=64) for a in range(2)]

        sorted_pairs = {}

        def doc_pairs(j):
            if j in sorted_pairs:
                return sorted_pairs[j][:]
            return doc_raw[j].bitcast(F32).rearrange("p (k m u) -> p k u m", k=KP, u=2)

        def sort_docs(j, copy):
            in_order = keep.tile([P, KP, 2, P], F32, name="in_order_%d" % j)
            copy(out=in_order[:], in_=doc_pairs(j))
            sorted_pairs[j] = in_order

        def turn_docs(j):
            bank = psum.tile([P, KP, 2, P], F32, name="turned", tag="aux")
            pairs = doc_pairs(j)
            for k in range(KP):
                for u in range(2):
                    nc.tensor.transpose(bank[:, k, u, :], pairs[:, k, u, :], ident[:])
            if j < HT:
                early_grouped[j] = keep.tile([P, KP, P, 2], F32, name="early_%d" % j, align_bytes=64)
                grouped = early_grouped[j][:]
            else:
                grouped = late_grouped[:, :, P * (j - HT) : P * (j - HT + 1), :]
            nc.scalar.copy(out=grouped, in_=bank[:].rearrange("p k u m -> p k m u"))

        def quantize_docs(half, lo, hi, grouped):
            for k in range(KP):
                nc.vector.quantize_mx(
                    out=doc_codes[half][:, k, lo:hi].bitcast(E4M3),
                    scales=doc_planes[half][:, k, lo:hi],
                    in_=grouped[:, k].rearrange("p m u -> p (m u)").bitcast(BF16),
                )

        def quantize_early_docs(j):
            quantize_docs(0, P * j, P * (j + 1), early_grouped[j])

        query_codes = [keep.tile([P, NQ], U32, name="query_codes_%d" % g, align_bytes=64) for g in range(TP)]
        query_planes = [keep.tile([P, NQ], U8, name="query_plane_%d" % g, align_bytes=64) for g in range(TP)]

        def group_queries(grouped, g, lo, hi):
            nc.gpsimd.tensor_scalar(
                out=grouped[:], in0=query_raw[g][:, :, lo:hi].rearrange("p t n -> p n t"),
                scalar1=1.0, scalar2=0.0, op0=ALU.mult, op1=ALU.add,
            )
            return grouped, g, lo, hi

        def quantize_queries(grouped, g, lo, hi):
            nc.vector.quantize_mx(
                out=query_codes[g][:, lo:hi].bitcast(E4M3), scales=query_planes[g][:, lo:hi],
                in_=grouped[:].rearrange("p n t -> p (n t)"),
            )

        inv_norm_col = keep.tile([P, DT], F32, name="inv_norm_col")
        inv_norm = keep.tile([P, DT, P], F32, name="inv_norm")
        inv_idf = keep.tile([P, SLOTS, TP], F32, name="inv_idf")

        def invert_norm():
            norm_root = keep.tile([P, DT], F32, name="norm_root")
            guess = keep.tile([P, DT], F32, name="guess")
            minus_one = keep.tile([P, DT], F32, name="minus_one")
            nc.scalar.activation(out=norm_root[:], in_=norm_col[:], func=ACT.Abs_reciprocal_sqrt)
            nc.scalar.activation(out=guess[:], in_=norm_root[:], func=ACT.Square)
            nc.vector.scalar_tensor_tensor(
                out=minus_one[:], in0=guess[:], scalar=-1.0, in1=norm_col[:], op0=ALU.mult, op1=ALU.mult
            )
            nc.vector.scalar_tensor_tensor(
                out=inv_norm_col[:], in0=minus_one[:], scalar=2.0, in1=guess[:], op0=ALU.add, op1=ALU.mult
            )

        def spread_norm(half):
            bank = psum.tile([P, HT, P], F32, name="norm_bank", tag="aux")
            for i in range(HT):
                j = HT * half + i
                nc.tensor.transpose(bank[:, i, :], inv_norm_col[:, j : j + 1].to_broadcast([P, P]), ident[:])
            nc.scalar.copy(out=inv_norm[:, HT * half : HT * (half + 1), :], in_=bank[:])

        def sort_idf():
            nc.scalar.copy(
                out=idf_rows[0:TP].rearrange("g t (m r) -> g t m r", r=4),
                in_=idf_raw[:].rearrange("g (m t r) -> g t m r", t=SLOTS, r=4),
            )

        def turn_idf():
            bank = psum.tile([P, SLOTS, P], F32, name="idf_bank", tag="aux")
            for t in range(SLOTS):
                nc.tensor.transpose(bank[:, t, :], idf_rows[:, t, :], ident[:])
            return bank

        logits = {}
        ratios = {}
        roots = {}
        weights = {}
        impacts = {}
        impact_mx = {}
        score_banks = {}

        def by_tiles(unit):
            return unit in (0, LAST)

        def e_passes(bank, unit, t, lo, hi):
            half, g = divmod(unit, TP)
            for k in range(KP):
                nc.tensor.matmul_mx(
                    out=bank,
                    lhsT=e_codes[g][:, k, t, :].bitcast(E2M1), lhsT_scale=e_planes[g][:, k, t, :],
                    rhs=doc_codes[half][:, k, lo:hi].bitcast(E4M3), rhs_scale=doc_planes[half][:, k, lo:hi],
                    start=(k == 0), stop=(k == KP - 1),
                )

        def first_product(unit, x):
            bank = psum.tile([P, W], F32, name="logit", tag="logit")
            if by_tiles(unit):
                for t in range(SLOTS):
                    e_passes(bank[:, P * t : P * (t + 1)], unit, t, P * x, P * (x + 1))
            else:
                e_passes(bank[:], unit, x, 0, W)
            logits[unit, x] = bank

        def ratio(unit, x):
            half = unit // TP
            if x == 0:
                ratios[unit] = work.tile([P, SLOTS, W], F32, name="ratio", bufs=LAG + 2)
            if by_tiles(unit):
                nc.vector.scalar_tensor_tensor(
                    out=ratios[unit][:, :, P * x : P * (x + 1)],
                    in0=logits[unit, x][:].rearrange("p (t m) -> p t m", t=SLOTS), scalar=0.0,
                    in1=inv_norm[:, HT * half + x, :].unsqueeze(1).to_broadcast([P, SLOTS, P]),
                    op0=ALU.max, op1=ALU.mult,
                )
            else:
                nc.vector.scalar_tensor_tensor(
                    out=ratios[unit][:, x, :], in0=logits[unit, x][:], scalar=0.0,
                    in1=inv_norm[:, HT * half : HT * (half + 1), :].rearrange("p j m -> p (j m)"),
                    op0=ALU.max, op1=ALU.mult,
                )

        def inverse_root(unit, t, lo, hi):
            g = unit % TP
            if unit not in roots:
                roots[unit] = work.tile([P, SLOTS, W], F32, name="root")
            nc.scalar.activation(
                out=roots[unit][:, t, lo:hi], in_=ratios[unit][:, t, lo:hi], func=ACT.Abs_reciprocal_sqrt,
                scale=inv_idf[:, t, g : g + 1], bias=inv_idf[:, t, g : g + 1],
            )

        def square(unit, t0, t1, lo, hi):
            if unit not in weights:
                weights[unit] = work.tile([P, SLOTS, W], F32, name="weight", bufs=LAG + 1)
            nc.scalar.activation(out=weights[unit][:, t0:t1, lo:hi], in_=roots[unit][:, t0:t1, lo:hi], func=ACT.Square)

        def impact(unit, lo, hi):
            if unit not in impacts:
                impacts[unit] = work.tile([P, W, SLOTS], BF16, name="impact", align_bytes=64)
            nc.vector.tensor_tensor(
                out=impacts[unit][:, lo:hi, :].rearrange("p (c e) t -> p c t e", e=2),
                in0=ratios[unit][:, :, lo:hi].rearrange("p t (c e) -> p c t e", e=2),
                in1=weights[unit][:, :, lo:hi].rearrange("p t (c e) -> p c t e", e=2),
                op=ALU.mult,
            )

        def quantize_impact(unit, lo, hi):
            half, g = divmod(unit, TP)
            codes = keep.tile([P, hi - lo], U32, name="impact_codes_%d_%d" % (unit, lo), align_bytes=64)
            plane = keep.tile([P, hi - lo], U8, name="impact_plane_%d_%d" % (unit, lo), align_bytes=64)
            nc.vector.quantize_mx(
                out=codes[:].bitcast(E5M2), scales=plane[:], in_=impacts[unit][:, lo:hi, :].rearrange("p n t -> p (n t)")
            )
            for first in range(lo, hi, P):
                cols = slice(first - lo, first - lo + P)
                impact_mx[HT * half + first // P, g] = (codes[:, cols], plane[:, cols])

        def finish_impacts(unit):
            for lo in (0, W // 2):
                impact(unit, lo, lo + W // 2)
            for lo in (0, W // 2):
                quantize_impact(unit, lo, lo + W // 2)

        def second_product(j, passes):
            if j not in score_banks:
                score_banks[j] = psum.tile([P, NQ], F32, name="score", tag="aux" if j < HT else "logit")
            for g in passes:
                codes, plane = impact_mx[j, g]
                nc.tensor.matmul_mx(
                    out=score_banks[j][:], lhsT=codes.bitcast(E5M2), lhsT_scale=plane,
                    rhs=query_codes[g][:].bitcast(E4M3), rhs_scale=query_planes[g][:],
                    start=(g == 0), stop=(g == TP - 1),
                )

        out_by_tile = out.rearrange("(p j) n -> p j n", j=DT)

        def store_scores(j):
            scores = work.tile([P, NQ], F32, name="scores", bufs=DT)
            nc.scalar.copy(out=scores[:], in_=score_banks[j][:])
            nc.sync.dma_start(out=out_by_tile[:, j, :], in_=scores[:])

        invert_norm()
        turn_docs(0)
        spread_norm(0)
        sort_codes(0)
        sort_docs(1, nc.vector.tensor_copy)
        turn_docs(1)
        sort_idf()
        sort_docs(3, nc.scalar.copy)
        sort_scales(scale_first, 0, 1)
        quantize_early_docs(0)
        first_product(0, 0)
        sort_docs(2, nc.vector.tensor_copy)
        turn_docs(2)
        quantize_early_docs(1)
        first_product(0, 1)
        turn_docs(3)
        sort_codes(1)
        ratio(0, 0)
        idf_bank = turn_idf()
        sort_scales(scale_rest, 1, TP - 1)
        quantize_early_docs(2)
        first_product(0, 2)
        ratio(0, 1)
        nc.vector.reciprocal(out=inv_idf[:], in_=idf_bank[:, :, 0:TP])
        for t in range(SLOTS):
            inverse_root(0, t, 0, W // 2)
        quantize_early_docs(3)
        first_product(0, 3)
        sort_codes(2)
        sort_codes(3)
        queries_0 = group_queries(gpsimd_tile([P, NQ, SLOTS], BF16), 0, 0, NQ)
        queries_1 = group_queries(keep.tile([P, NQ, SLOTS], BF16, name="queries_1", align_bytes=64), 1, 0, NQ)
        ratio(0, 2)
        first_product(1, 0)
        first_product(1, 1)
        square(0, 0, SLOTS, 0, W // 2)
        ratio(0, 3)
        first_product(1, 2)
        first_product(1, 3)
        for t in range(SLOTS):
            inverse_root(0, t, W // 2, W)
        square(0, 0, SLOTS, W // 2, W)

        for unit in range(1, UNITS):
            for x in range(SLOTS):
                ratio(unit, x)
                if unit < LAST:
                    first_product(unit + 1, x)
                    inverse_root(unit, x, 0, W)
                else:
                    for t in range(SLOTS):
                        inverse_root(unit, t, P * x, P * (x + 1))
                    if x > 0:
                        square(unit, 0, SLOTS, P * (x - 1), P * x)
                if unit == TP + 1:
                    second_product(x, range(0, 2))
                if unit == LAST:
                    second_product(x, range(2, TP))
            if unit == 1:
                for j in range(HT, DT):
                    turn_docs(j)
            if unit < LAST:
                square(unit, 0, 2, 0, W)
                if unit == 2:
                    spread_norm(1)
                square(unit, 2, SLOTS, 0, W)
            else:
                square(unit, 0, SLOTS, W - P, W)
                for j in range(HT):
                    store_scores(j)

            if unit >= LAG:
                finish_impacts(unit - LAG)
            if unit == LAG:
                quantize_queries(*queries_1)
                quantize_docs(1, 0, W, late_grouped)
                quantize_queries(*queries_0)
            if LAG < unit <= LAG + len(QUERY_HALVES):
                quantize_queries(*query_half)
            if LAG <= unit < LAG + len(QUERY_HALVES):
                g, lo = QUERY_HALVES[unit - LAG]
                query_half = group_queries(gpsimd_tile([P, NQ // 2, SLOTS], BF16), g, lo, lo + NQ // 2)

        for i in range(HT):
            second_product(HT + i, range(0, 2))
        finish_impacts(LAST - 1)
        impact(LAST, 0, P)
        for i in range(HT):
            second_product(HT + i, [TP - 2])
        for i in range(HT):
            if i + 1 < HT:
                impact(LAST, P * (i + 1), P * (i + 2))
            quantize_impact(LAST, P * i, P * (i + 1))
            second_product(HT + i, [TP - 1])
            store_scores(HT + i)
